import numpy as np
import ml_dtypes


def mxq(x, axis, fmt="e4m3"):
    dtype, down = {"e4m3": (ml_dtypes.float8_e4m3fn, 7), "e5m2": (ml_dtypes.float8_e5m2, 14)}[fmt]
    v = np.moveaxis(np.asarray(x, np.float32).astype(ml_dtypes.bfloat16).astype(np.float64), axis, -1)
    blocks = v.reshape(v.shape[:-1] + (-1, 32))
    amax = np.abs(blocks).max(-1, keepdims=True)
    byte = np.maximum(np.where(amax > 0, np.frexp(amax)[1] - 1 + 127, 0) - down, 1)
    scale = np.exp2(byte - 127.0)
    codes = (blocks / scale).astype(np.float32).astype(dtype).astype(np.float64)
    return np.moveaxis((codes * scale).reshape(v.shape), -1, axis)


WIDE = False


def mx_kscale(k):
    if not WIDE:
        return np.ones(k)
    levels = np.array([10, -10, 5, -5, 0])
    if k % 512:
        return np.exp2(np.random.permutation(np.resize(levels, k // 32))).repeat(32)
    a = np.empty((k // 512, 16))
    for p in range(k // 512):
        a[p, :8] = np.random.permutation(np.resize(levels, 8))
        for g in range(8):
            far = levels[np.abs(levels - a[p, g]) >= 10]
            a[p, g + 8] = far[np.random.randint(len(far))]
    return np.exp2(a.ravel()).repeat(32)


BF16 = ml_dtypes.bfloat16


def bf(x):
    return np.asarray(x, np.float32).astype(BF16)


def f64(x):
    return np.asarray(x).astype(np.float64)


E2M1 = np.array([0.0, 0.5, 1.0, 1.5, 2.0, 3.0, 4.0, 6.0, -0.0, -0.5, -1.0, -1.5, -2.0, -3.0, -4.0, -6.0])


def pack_weight(w, fmt):
    k, n = w.shape
    w = f64(bf(w)).reshape(k // 32, 32, n)
    amax = np.abs(w).max(1)
    if fmt == "e4m3":
        byte = np.frexp(amax)[1] - 1 + 127 - 7
    else:
        mant, ex = np.frexp(amax / 6.0)
        byte = np.where(mant > 0.5, ex, ex - 1) + 127
    byte = np.clip(np.where(amax > 0, byte, 1), 1, 254)
    scaled = (w * np.exp2(127.0 - byte)[:, None, :]).reshape(k, n).astype(np.float32)
    by_word = np.ascontiguousarray(scaled.reshape(k // 512, 128, 4, n).transpose(0, 1, 3, 2))
    if fmt == "e4m3":
        words = by_word.astype(ml_dtypes.float8_e4m3fn).view(np.uint8)
    else:
        c = by_word.astype(ml_dtypes.float4_e2m1fn).view(np.uint8) & 0xF
        words = c[..., 0::2] | (c[..., 1::2] << 4)
    return np.ascontiguousarray(words), np.ascontiguousarray(byte.astype(np.uint8).reshape(k // 512, 16, n))


def unpack_weight(words, scales, fmt):
    g, p, n, _ = words.shape
    if fmt == "e4m3":
        vals = np.ascontiguousarray(words).view(ml_dtypes.float8_e4m3fn).astype(np.float64)
    else:
        nib = np.empty((g, p, n, 4), np.uint8)
        nib[..., 0::2] = words & 0xF
        nib[..., 1::2] = words >> 4
        vals = E2M1[nib]
    vals = vals * np.repeat(np.exp2(scales.astype(np.float64) - 127.0), 8, axis=1)[..., None]
    return vals.transpose(0, 1, 3, 2).reshape(g * 512, n)

def planes(Y):
    n, m = Y.shape
    b = f64(bf(Y)).reshape(n // 32, 32, m)
    amax = np.abs(b).max(1)
    byte = np.clip(np.where(amax > 0, np.frexp(amax)[1] - 1 + 127 - 7, 1), 1, 254)
    codes = (b * np.exp2(127.0 - byte)[:, None, :]).reshape(n, m).astype(np.float32).astype(ml_dtypes.float8_e4m3fn).view(np.uint8)
    words = codes.reshape(n // 512, 128, 4, m).transpose(0, 1, 3, 2)
    return np.ascontiguousarray(words), np.ascontiguousarray(byte.astype(np.uint8).reshape(n // 512, 16, m))


B, N, D, A, L = 4, 512, 512, 512, 1024


def setup_inputs():
    s, t = mx_kscale(D), mx_kscale(A)
    h = bf(np.random.standard_normal((B, N, D)) * s)
    w_words, w_scales = pack_weight(np.random.standard_normal((D, A)) / np.sqrt(D) / s[:, None], "e4m3")
    g = bf((1.0 + 0.1 * np.random.standard_normal(A)) * t)
    u_words, u_scales = pack_weight((1.5 * np.random.standard_normal((L, A)) / np.sqrt(A) / t[None, :]).T, "e4m3")
    beta_words, beta_scales = pack_weight((np.random.standard_normal((L, D)) / np.sqrt(D) / s[None, :]).T, "e4m3")
    c = bf(0.3 * np.random.standard_normal(L))
    return {"h": h,
            "w_words": w_words,
            "w_scales": w_scales,
            "g": g,
            "u_words": u_words,
            "u_scales": u_scales,
            "beta_words": beta_words,
            "beta_scales": beta_scales,
            "c": c}


def softmax_over_tokens(v):
    shifted = v - np.max(v, axis=1, keepdims=True)
    ex = np.exp(shifted)
    return ex / np.sum(ex, axis=1, keepdims=True)


def core(h, w_words, w_scales, g, u_words, u_scales, beta_words, beta_scales, c):
    n_tokens = h.shape[1]
    hq = mxq(f64(h), 2, "e4m3")
    z = f64(g) * np.tanh(hq @ unpack_weight(w_words, w_scales, "e4m3"))
    scores = mxq(z, 2, "e4m3") @ unpack_weight(u_words, u_scales, "e4m3")
    att = softmax_over_tokens(scores)
    p = hq @ unpack_weight(beta_words, beta_scales, "e4m3")
    return n_tokens * att * p + f64(c)


def reference(h, w_words, w_scales, g, u_words, u_scales, beta_words, beta_scales, c):
    R_out = core(h, w_words, w_scales, g, u_words, u_scales, beta_words, beta_scales, c)
    words, scales = planes(np.moveaxis(R_out, 1, 0).reshape(512, -1))
    return R_out, words, scales

@@ -1,0 +1,329 @@
+from contextlib import ExitStack
+
+import concourse.mybir as mybir
+from concourse.masks import make_identity
+
+B, T, D, A, L = 4, 512, 512, 512, 1024
+P = 128
+NT = T // P
+NL = L // P
+
+F32 = mybir.dt.float32
+BF16 = mybir.dt.bfloat16
+I32 = mybir.dt.int32
+U8 = mybir.dt.uint8
+FP8X4 = mybir.dt.float8_e4m3fn_x4
+ACT = mybir.ActivationFunctionType
+ALU = mybir.AluOpType
+AX = mybir.AxisListType
+
+PB = {"s": 3, "p": 2, "t": 2, "z": 1}
+FLOPS = 2 * B * T * (D * A + A * L + D * L)
+
+
+def tile_laatlabelwisetokenevidence_x2_kernel(
+    tc, h, w_words, w_scales, g, u_words, u_scales, beta_words, beta_scales, c, out_0, out_1, out_2
+):
+    nc = tc.nc
+    out_words = out_1[0].rearrange("p m t -> p (m t)")
+
+    with ExitStack() as ctx:
+        const = ctx.enter_context(tc.tile_pool(name="const", bufs=1))
+        stage = ctx.enter_context(tc.tile_pool(name="stage", bufs=4))
+        keep = ctx.enter_context(tc.tile_pool(name="keep", bufs=2))
+        stats = ctx.enter_context(tc.tile_pool(name="stats", bufs=4))
+        psum = ctx.enter_context(tc.psum_pool(name="psum", bufs=2))
+        ctx.enter_context(tc.manual_schedule())
+
+        h_sb = {}
+        for b in range(B):
+            for hf in range(2):
+                h_sb[b, hf] = const.tile([P, 2, D], BF16, name="h_sb_%d_%d" % (b, hf), align_bytes=64)
+
+        def load_h(b, hf):
+            src = h[b].rearrange("(p t) d -> p t d", t=NT)
+            nc.sync.dma_start(out=h_sb[b, hf][:], in_=src[:, 2 * hf : 2 * hf + 2, :])
+
+        warm = const.tile([P, 1], F32, name="warm")
+        nc.vector.memset(warm[:], 0.0)
+        w_raw = const.tile([P, A], I32, name="w_raw", align_bytes=64)
+        ws_raw = const.tile([P, A], U8, name="ws_raw", align_bytes=64)
+        u_sb = const.tile([P, L], I32, name="u_sb", align_bytes=64)
+        us_sb = const.tile([P, L], U8, name="us_sb", align_bytes=64)
+        b_sb = const.tile([P, L], I32, name="b_sb", align_bytes=64)
+        bs_sb = const.tile([P, L], U8, name="bs_sb", align_bytes=64)
+        g_bf = const.tile([P, 4], BF16, name="g_bf")
+        c_rows = const.tile([P, P], BF16, name="c_rows", align_bytes=64)
+        nc.vector.memset(ws_raw[:].bitcast(I32), 0)
+        nc.vector.memset(us_sb[:].bitcast(I32), 0)
+        nc.vector.memset(bs_sb[:].bitcast(I32), 0)
+        nc.vector.memset(c_rows[:], 0.0)
+
+        load_h(0, 0)
+        nc.sync.dma_start(out=w_raw[:], in_=w_words[0].rearrange("p n t -> p (n t)").bitcast(I32))
+        load_h(0, 1)
+        for r in range(4):
+            nc.scalar.dma_start(out=ws_raw[r:P:32, :].bitcast(I32), in_=w_scales[0, r:16:4, :].bitcast(I32))
+        nc.scalar.dma_start(out=g_bf[:], in_=g.rearrange("(p t) -> p t", t=4))
+        nc.scalar.dma_start(out=c_rows[0:NL, :], in_=c.rearrange("(j p) -> j p", p=P))
+        nc.sync.dma_start(out=u_sb[:], in_=u_words[0].rearrange("p n t -> p (n t)").bitcast(I32))
+        for r in range(4):
+            nc.sync.dma_start(out=us_sb[r:P:32, :].bitcast(I32), in_=u_scales[0, r:16:4, :].bitcast(I32))
+        nc.sync.dma_start(out=b_sb[:], in_=beta_words[0].rearrange("p n t -> p (n t)").bitcast(I32))
+        for r in range(4):
+            nc.sync.dma_start(out=bs_sb[r:P:32, :].bitcast(I32), in_=beta_scales[0, r:16:4, :].bitcast(I32))
+        for b in range(1, B):
+            load_h(b, 0)
+            load_h(b, 1)
+
+        nc.scalar.activation(out=warm[:], in_=warm[:], func=ACT.Exp)
+        ident = const.tile([P, P], F32, name="ident", align_bytes=64)
+        make_identity(nc, ident[:])
+        w_sb = const.tile([P, 4, P], I32, name="w_sb", align_bytes=64)
+        ws_sb = const.tile([P, 4, P], U8, name="ws_sb", align_bytes=64)
+        g_sb = const.tile([P, 4], F32, name="g_sb")
+        c_f32 = const.tile([P, P], F32, name="c_f32", align_bytes=64)
+        c_sb = const.tile([P, NL], F32, name="c_sb")
+
+        def prep_w():
+            nc.vector.tensor_copy(out=w_sb[:], in_=w_raw[:].rearrange("p (m t) -> p t m", t=4))
+            nc.vector.tensor_copy(out=ws_sb[:], in_=ws_raw[:].rearrange("p (m t) -> p t m", t=4))
+            nc.vector.tensor_copy(out=g_sb[:], in_=g_bf[:])
+
+        def prep_c():
+            nc.vector.tensor_copy(out=c_f32[:], in_=c_rows[:])
+            ct = psum.tile([P, P], F32, name="ct", tag="t", bufs=PB["t"])
+            nc.tensor.transpose(ct[:], c_f32[:], ident[:])
+            nc.vector.tensor_copy(out=c_sb[:], in_=ct[:, 0:NL])
+
+        h_codes, h_scales, z_codes, z_scales, z_t, z_b = {}, {}, {}, {}, {}, {}
+        hg = {}
+
+        def h_turn(b, i, tag):
+            if i == 0:
+                h_codes[b] = keep.tile([P, T], I32, name="h_codes", tag="h_codes", align_bytes=64)
+                h_scales[b] = keep.tile([P, T], U8, name="h_scales", tag="h_scales", align_bytes=64)
+            words = h_sb[b, i // 2][:].bitcast(F32)
+            bank = psum.tile([P, 2, P], F32, name="ht", tag=tag, bufs=PB[tag])
+            for e in range(2):
+                nc.tensor.transpose(bank[:, e, :], words[:, i % 2, e : D // 2 : 2], ident[:])
+            hg[b, i] = stage.tile([P, P, 4], BF16, name="hg", tag="hg", align_bytes=64)
+            nc.scalar.copy(out=hg[b, i][:].bitcast(F32), in_=bank[:].rearrange("m e p -> m p e"))
+
+        def h_quant(b, i):
+            cols = slice(P * i, P * (i + 1))
+            nc.vector.quantize_mx(
+                out=h_codes[b][:, cols].bitcast(FP8X4),
+                scales=h_scales[b][:, cols],
+                in_=hg[b, i][:].rearrange("m p t -> m (p t)"),
+            )
+
+        def z_mm(b, i, tag):
+            cols = slice(P * i, P * (i + 1))
+            bank = psum.tile([P, 4, P], F32, name="zp", tag=tag, bufs=PB[tag])
+            for t in range(4):
+                nc.tensor.matmul_mx(
+                    out=bank[:, t, :],
+                    lhsT=w_sb[:, t, :].bitcast(FP8X4),
+                    lhsT_scale=ws_sb[:, t, :],
+                    rhs=h_codes[b][:, cols].bitcast(FP8X4),
+                    rhs_scale=h_scales[b][:, cols],
+                    start=True,
+                    stop=True,
+                )
+            z_t[b, i] = stage.tile([P, P, 4], F32, name="z_t", tag="z_t")
+            nc.scalar.activation(out=z_t[b, i][:], in_=bank[:].rearrange("m t n -> m n t"), func=ACT.Tanh)
+
+        def z_gain(b, i, eng):
+            z_b[b, i] = stage.tile([P, P, 4], BF16, name="z_b", tag="z_b", align_bytes=64)
+            eng.tensor_tensor(
+                out=z_b[b, i][:],
+                in0=z_t[b, i][:],
+                in1=g_sb[:].unsqueeze(1).to_broadcast([P, P, 4]),
+                op=ALU.mult,
+            )
+
+        def z_quant(b, i):
+            if i == 0:
+                z_codes[b] = keep.tile([P, T], I32, name="z_codes", tag="z_codes", align_bytes=64)
+                z_scales[b] = keep.tile([P, T], U8, name="z_scales", tag="z_scales", align_bytes=64)
+            cols = slice(P * i, P * (i + 1))
+            nc.vector.quantize_mx(
+                out=z_codes[b][:, cols].bitcast(FP8X4),
+                scales=z_scales[b][:, cols],
+                in_=z_b[b, i][:].rearrange("m p t -> m (p t)"),
+            )
+
+        NU = B * NL
+        s_ps, p_ps, neg, dsum, rinv, ex, vt, wt = {}, {}, {}, {}, {}, {}, {}, {}
+        groups = [list(range(4 * q, 4 * q + 4)) for q in range(NU // 4 - 1)]
+        groups += [[NU - 4, NU - 3], [NU - 2], [NU - 1]]
+        group_of = {}
+        for gi in range(len(groups)):
+            for u in groups[gi]:
+                group_of[u] = gi
+        y32, y16 = {}, {}
+        o_scales = const.tile([P, B * L], U8, name="o_scales", align_bytes=64)
+
+        def s_mm(u):
+            b, j = divmod(u, NL)
+            cols = slice(P * j, P * (j + 1))
+            s_ps[u] = psum.tile([P, T], F32, name="s_ps", tag="s", bufs=PB["s"])
+            nc.tensor.matmul_mx(
+                out=s_ps[u][:],
+                lhsT=u_sb[:, cols].bitcast(FP8X4),
+                lhsT_scale=us_sb[:, cols],
+                rhs=z_codes[b][:].bitcast(FP8X4),
+                rhs_scale=z_scales[b][:],
+                start=True,
+                stop=True,
+            )
+
+        def p_mm(u):
+            b, j = divmod(u, NL)
+            cols = slice(P * j, P * (j + 1))
+            p_ps[u] = psum.tile([P, T], F32, name="p_ps", tag="p", bufs=PB["p"])
+            nc.tensor.matmul_mx(
+                out=p_ps[u][:],
+                lhsT=b_sb[:, cols].bitcast(FP8X4),
+                lhsT_scale=bs_sb[:, cols],
+                rhs=h_codes[b][:].bitcast(FP8X4),
+                rhs_scale=h_scales[b][:],
+                start=True,
+                stop=True,
+            )
+
+        def vmax(u):
+            neg[u] = stats.tile([P, 1], F32, name="neg", tag="neg")
+            nc.vector.tensor_reduce(out=neg[u][:], in_=s_ps[u][:], axis=AX.X, op=ALU.max, negate=True)
+
+        def sexp(u):
+            ex[u] = stage.tile([P, T], F32, name="ex", tag="ex")
+            dsum[u] = stats.tile([P, 1], F32, name="dsum", tag="dsum")
+            nc.scalar.activation(
+                out=ex[u][:], in_=s_ps[u][:], func=ACT.Exp, bias=neg[u][:], accum_out=dsum[u][:]
+            )
+
+        def vmul(u):
+            rinv[u] = stats.tile([P, 1], F32, name="rinv", tag="rinv")
+            nc.vector.reciprocal(out=rinv[u][:], in_=dsum[u][:])
+            vt[u] = stage.tile([P, T], F32, name="vt", tag="vt")
+            nc.vector.scalar_tensor_tensor(
+                out=vt[u][:], in0=p_ps[u][:], scalar=float(T), in1=ex[u][:], op0=ALU.mult, op1=ALU.mult
+            )
+
+        def affine(u):
+            wt[u] = stage.tile([P, T], F32, name="wt", tag="wt")
+            j = u % NL
+            nc.gpsimd.tensor_scalar(
+                out=wt[u][:], in0=vt[u][:], scalar1=rinv[u][:], scalar2=c_sb[:, j : j + 1], op0=ALU.mult, op1=ALU.add
+            )
+
+        def turn(u):
+            gi = group_of[u]
+            n = len(groups[gi])
+            k = u - groups[gi][0]
+            if k == 0:
+                y32[gi] = stage.tile([P, 4, n * P], F32, name="y32", tag="y32")
+                y16[gi] = stage.tile([P, n * P, 4], BF16, name="y16", tag="y16", align_bytes=64)
+            bank = psum.tile([P, 4, P], F32, name="tp", tag="t", bufs=PB["t"])
+            for t in range(4):
+                nc.tensor.transpose(bank[:, t, :], wt[u][:, P * t : P * (t + 1)], ident[:])
+            nc.scalar.copy(out=y32[gi][:, :, P * k : P * (k + 1)], in_=bank[:])
+
+        def round_out(u):
+            gi = group_of[u]
+            k = u - groups[gi][0]
+            cols = slice(P * k, P * (k + 1))
+            nc.vector.tensor_copy(out=y16[gi][:, cols, :], in_=y32[gi][:, :, cols].rearrange("p t l -> p l t"))
+
+        def store_y(gi):
+            u0, n = groups[gi][0], len(groups[gi])
+            b, j = divmod(u0, NL)
+            dst = out_0[b].rearrange("(p t) l -> p t l", t=4)
+            nc.sync.dma_start(out=dst[:, :, P * j : P * (j + n)], in_=y32[gi][:])
+
+        def quant_out(gi):
+            u0, n = groups[gi][0], len(groups[gi])
+            m0, m1 = P * u0, P * (u0 + n)
+            o_codes = stage.tile([P, n * P], I32, name="o_codes", tag="o_codes", align_bytes=64)
+            nc.vector.quantize_mx(
+                out=o_codes[:].bitcast(FP8X4),
+                scales=o_scales[:, m0:m1],
+                in_=y16[gi][:].rearrange("p l t -> p (l t)"),
+            )
+            nc.sync.dma_start(out=out_words[:, 4 * m0 : 4 * m1].bitcast(I32), in_=o_codes[:])
+            u1 = u0 + n
+            if u1 % NL == 0:
+                m0 = P * (u1 - NL)
+                for q in range(4):
+                    nc.sync.dma_start(
+                        out=out_2[0, 4 * q : 4 * q + 4, m0:m1].bitcast(I32),
+                        in_=o_scales[32 * q : 32 * q + 4, m0:m1].bitcast(I32),
+                    )
+
+        h_turn(0, 0, "t")
+        h_turn(0, 1, "t")
+        prep_w()
+        h_quant(0, 0)
+        z_mm(0, 0, "z")
+        h_quant(0, 1)
+        z_mm(0, 1, "s")
+        h_turn(0, 2, "t")
+        z_gain(0, 0, nc.vector)
+        h_quant(0, 2)
+        z_mm(0, 2, "s")
+        z_quant(0, 0)
+        h_turn(0, 3, "t")
+        z_gain(0, 1, nc.vector)
+        h_quant(0, 3)
+        z_mm(0, 3, "s")
+        z_quant(0, 1)
+        prep_c()
+        z_gain(0, 2, nc.vector)
+        z_gain(0, 3, nc.vector)
+        z_quant(0, 2)
+        z_quant(0, 3)
+        s_mm(0)
+        s_mm(1)
+        p_mm(0)
+        vmax(0)
+        sexp(0)
+
+        for k in range(NU + 5):
+            b, j = divmod(k, NL)
+            nb = b + 1
+            if k + 1 < NU:
+                vmax(k + 1)
+            if 0 <= k - 2 < NU:
+                turn(k - 2)
+            if k + 2 < NU:
+                s_mm(k + 2)
+            if k + 1 < NU:
+                p_mm(k + 1)
+            if nb < B:
+                if 0 <= j - 1 < 4:
+                    z_mm(nb, j - 1, "z")
+                if j < 4:
+                    h_turn(nb, j, "t")
+                if 0 <= j - 2 < 4:
+                    z_gain(nb, j - 2, nc.gpsimd)
+            if k + 1 < NU:
+                sexp(k + 1)
+            if k < NU:
+                vmul(k)
+                affine(k)
+            if 0 <= k - 3 < NU:
+                round_out(k - 3)
+                gi = group_of[k - 3]
+                if groups[gi][-1] == k - 3:
+                    store_y(gi)
+            if nb < B:
+                if j < 4:
+                    h_quant(nb, j)
+                if 0 <= j - 2 < 4:
+                    z_quant(nb, j - 2)
+            if 0 <= k - 4 < NU:
+                gi = group_of[k - 4]
+                if groups[gi][-1] == k - 4:
+                    quant_out(gi)

@@ -7,6 +7,7 @@ B, T, D, A, L = 4, 512, 512, 512, 1024
 P = 128
 NT = T // P
 NL = L // P
+NU = B * NL
 
 F32 = mybir.dt.float32
 BF16 = mybir.dt.bfloat16
@@ -17,7 +18,7 @@ ACT = mybir.ActivationFunctionType
 ALU = mybir.AluOpType
 AX = mybir.AxisListType
 
-PB = {"s": 3, "p": 2, "t": 2, "z": 1}
+BANKS = {"s": 3, "p": 2, "t": 2, "z": 1}
 FLOPS = 2 * B * T * (D * A + A * L + D * L)
 
 
@@ -30,7 +31,6 @@ def tile_laatlabelwisetokenevidence_x2_kernel(
     with ExitStack() as ctx:
         const = ctx.enter_context(tc.tile_pool(name="const", bufs=1))
         stage = ctx.enter_context(tc.tile_pool(name="stage", bufs=4))
-        keep = ctx.enter_context(tc.tile_pool(name="keep", bufs=2))
         stats = ctx.enter_context(tc.tile_pool(name="stats", bufs=4))
         psum = ctx.enter_context(tc.psum_pool(name="psum", bufs=2))
         ctx.enter_context(tc.manual_schedule())
@@ -38,11 +38,12 @@ def tile_laatlabelwisetokenevidence_x2_kernel(
         h_sb = {}
         for b in range(B):
             for hf in range(2):
-                h_sb[b, hf] = const.tile([P, 2, D], BF16, name="h_sb_%d_%d" % (b, hf), align_bytes=64)
+                h_sb[2 * b + hf] = const.tile([P, 2, D], BF16, name="h_sb_%d_%d" % (b, hf), align_bytes=64)
 
-        def load_h(b, hf):
+        def load_h(hh):
+            b, hf = divmod(hh, 2)
             src = h[b].rearrange("(p t) d -> p t d", t=NT)
-            nc.sync.dma_start(out=h_sb[b, hf][:], in_=src[:, 2 * hf : 2 * hf + 2, :])
+            nc.sync.dma_start(out=h_sb[hh][:], in_=src[:, 2 * hf : 2 * hf + 2, :])
 
         warm = const.tile([P, 1], F32, name="warm")
         nc.vector.memset(warm[:], 0.0)
@@ -53,28 +54,31 @@ def tile_laatlabelwisetokenevidence_x2_kernel(
         b_sb = const.tile([P, L], I32, name="b_sb", align_bytes=64)
         bs_sb = const.tile([P, L], U8, name="bs_sb", align_bytes=64)
         g_bf = const.tile([P, 4], BF16, name="g_bf")
-        c_rows = const.tile([P, P], BF16, name="c_rows", align_bytes=64)
+        c_row = const.tile([P, L], BF16, name="c_row", align_bytes=64)
+        spread = const.tile([P, P], BF16, name="spread", align_bytes=64)
         nc.vector.memset(ws_raw[:].bitcast(I32), 0)
         nc.vector.memset(us_sb[:].bitcast(I32), 0)
         nc.vector.memset(bs_sb[:].bitcast(I32), 0)
-        nc.vector.memset(c_rows[:], 0.0)
+        nc.vector.memset(c_row[:], 0.0)
+        nc.vector.memset(spread[:], 1.0 / T)
 
-        load_h(0, 0)
+        def load_scales(eng, dst, src):
+            for r in range(4):
+                eng.dma_start(out=dst[r:P:32, :].bitcast(I32), in_=src[0, r:16:4, :].bitcast(I32))
+
+        load_h(0)
         nc.sync.dma_start(out=w_raw[:], in_=w_words[0].rearrange("p n t -> p (n t)").bitcast(I32))
-        load_h(0, 1)
-        for r in range(4):
-            nc.scalar.dma_start(out=ws_raw[r:P:32, :].bitcast(I32), in_=w_scales[0, r:16:4, :].bitcast(I32))
+        load_h(1)
+        load_scales(nc.scalar, ws_raw, w_scales)
         nc.scalar.dma_start(out=g_bf[:], in_=g.rearrange("(p t) -> p t", t=4))
-        nc.scalar.dma_start(out=c_rows[0:NL, :], in_=c.rearrange("(j p) -> j p", p=P))
+        load_h(2)
         nc.sync.dma_start(out=u_sb[:], in_=u_words[0].rearrange("p n t -> p (n t)").bitcast(I32))
-        for r in range(4):
-            nc.sync.dma_start(out=us_sb[r:P:32, :].bitcast(I32), in_=u_scales[0, r:16:4, :].bitcast(I32))
+        load_scales(nc.sync, us_sb, u_scales)
         nc.sync.dma_start(out=b_sb[:], in_=beta_words[0].rearrange("p n t -> p (n t)").bitcast(I32))
-        for r in range(4):
-            nc.sync.dma_start(out=bs_sb[r:P:32, :].bitcast(I32), in_=beta_scales[0, r:16:4, :].bitcast(I32))
-        for b in range(1, B):
-            load_h(b, 0)
-            load_h(b, 1)
+        load_scales(nc.sync, bs_sb, beta_scales)
+        nc.sync.dma_start(out=c_row[0:1, :], in_=c.rearrange("(o l) -> o l", o=1))
+        for hh in range(3, 2 * B):
+            load_h(hh)
 
         nc.scalar.activation(out=warm[:], in_=warm[:], func=ACT.Exp)
         ident = const.tile([P, P], F32, name="ident", align_bytes=64)
@@ -82,48 +86,47 @@ def tile_laatlabelwisetokenevidence_x2_kernel(
         w_sb = const.tile([P, 4, P], I32, name="w_sb", align_bytes=64)
         ws_sb = const.tile([P, 4, P], U8, name="ws_sb", align_bytes=64)
         g_sb = const.tile([P, 4], F32, name="g_sb")
-        c_f32 = const.tile([P, P], F32, name="c_f32", align_bytes=64)
-        c_sb = const.tile([P, NL], F32, name="c_sb")
 
         def prep_w():
             nc.vector.tensor_copy(out=w_sb[:], in_=w_raw[:].rearrange("p (m t) -> p t m", t=4))
             nc.vector.tensor_copy(out=ws_sb[:], in_=ws_raw[:].rearrange("p (m t) -> p t m", t=4))
             nc.vector.tensor_copy(out=g_sb[:], in_=g_bf[:])
 
-        def prep_c():
-            nc.vector.tensor_copy(out=c_f32[:], in_=c_rows[:])
-            ct = psum.tile([P, P], F32, name="ct", tag="t", bufs=PB["t"])
-            nc.tensor.transpose(ct[:], c_f32[:], ident[:])
-            nc.vector.tensor_copy(out=c_sb[:], in_=ct[:, 0:NL])
+        h_codes, h_scales, z_codes, z_scales = {}, {}, {}, {}
+        for b in range(B):
+            h_codes[b] = const.tile([P, T], I32, name="h_codes_%d" % b, align_bytes=64)
+            h_scales[b] = const.tile([P, T], U8, name="h_scales_%d" % b, align_bytes=64)
+            z_codes[b] = const.tile([P, T], I32, name="z_codes_%d" % b, align_bytes=64)
+            z_scales[b] = const.tile([P, T], U8, name="z_scales_%d" % b, align_bytes=64)
+        h_bank, h_il, z_bank, z_t, z_b = {}, {}, {}, {}, {}
 
-        h_codes, h_scales, z_codes, z_scales, z_t, z_b = {}, {}, {}, {}, {}, {}
-        hg = {}
+        def h_turn(hh, tag):
+            words = h_sb[hh][:].bitcast(F32)
+            h_bank[hh] = psum.tile([P, 2, 2, P], F32, name="h_bank", tag=tag, bufs=BANKS[tag])
+            for i in range(2):
+                for e in range(2):
+                    nc.tensor.transpose(h_bank[hh][:, i, e, :], words[:, i, e : D // 2 : 2], ident[:])
 
-        def h_turn(b, i, tag):
-            if i == 0:
-                h_codes[b] = keep.tile([P, T], I32, name="h_codes", tag="h_codes", align_bytes=64)
-                h_scales[b] = keep.tile([P, T], U8, name="h_scales", tag="h_scales", align_bytes=64)
-            words = h_sb[b, i // 2][:].bitcast(F32)
-            bank = psum.tile([P, 2, P], F32, name="ht", tag=tag, bufs=PB[tag])
-            for e in range(2):
-                nc.tensor.transpose(bank[:, e, :], words[:, i % 2, e : D // 2 : 2], ident[:])
-            hg[b, i] = stage.tile([P, P, 4], BF16, name="hg", tag="hg", align_bytes=64)
-            nc.scalar.copy(out=hg[b, i][:].bitcast(F32), in_=bank[:].rearrange("m e p -> m p e"))
+        def h_copy(hh):
+            h_il[hh] = stage.tile([P, 2, P, 4], BF16, name="h_il", tag="h_il", bufs=2, align_bytes=64)
+            nc.scalar.copy(out=h_il[hh][:].bitcast(F32), in_=h_bank[hh][:].rearrange("m i e p -> m i p e"))
 
-        def h_quant(b, i):
-            cols = slice(P * i, P * (i + 1))
+        def h_quant(hh):
+            b, hf = divmod(hh, 2)
+            cols = slice(2 * P * hf, 2 * P * (hf + 1))
             nc.vector.quantize_mx(
                 out=h_codes[b][:, cols].bitcast(FP8X4),
                 scales=h_scales[b][:, cols],
-                in_=hg[b, i][:].rearrange("m p t -> m (p t)"),
+                in_=h_il[hh][:].rearrange("m i p t -> m (i p t)"),
             )
 
-        def z_mm(b, i, tag):
-            cols = slice(P * i, P * (i + 1))
-            bank = psum.tile([P, 4, P], F32, name="zp", tag=tag, bufs=PB[tag])
+        def z_mm(i, tag):
+            b, t_i = divmod(i, NT)
+            cols = slice(P * t_i, P * (t_i + 1))
+            z_bank[i] = psum.tile([P, 4, P], F32, name="z_bank", tag=tag, bufs=BANKS[tag])
             for t in range(4):
                 nc.tensor.matmul_mx(
-                    out=bank[:, t, :],
+                    out=z_bank[i][:, t, :],
                     lhsT=w_sb[:, t, :].bitcast(FP8X4),
                     lhsT_scale=ws_sb[:, t, :],
                     rhs=h_codes[b][:, cols].bitcast(FP8X4),
@@ -131,44 +134,47 @@ def tile_laatlabelwisetokenevidence_x2_kernel(
                     start=True,
                     stop=True,
                 )
-            z_t[b, i] = stage.tile([P, P, 4], F32, name="z_t", tag="z_t")
-            nc.scalar.activation(out=z_t[b, i][:], in_=bank[:].rearrange("m t n -> m n t"), func=ACT.Tanh)
 
-        def z_gain(b, i, eng):
-            z_b[b, i] = stage.tile([P, P, 4], BF16, name="z_b", tag="z_b", align_bytes=64)
+        def z_tanh(i):
+            z_t[i] = stage.tile([P, P, 4], F32, name="z_t", tag="z_t")
+            nc.scalar.activation(out=z_t[i][:], in_=z_bank[i][:].rearrange("m t n -> m n t"), func=ACT.Tanh)
+
+        def bf16_tile(eng):
+            tag = "by_gpsimd" if eng is nc.gpsimd else "by_vector"
+            return stage.tile([P, P, 4], BF16, name=tag, tag=tag, bufs=2 if eng is nc.gpsimd else 4, align_bytes=64)
+
+        def z_gain(i, eng):
+            z_b[i] = bf16_tile(eng)
             eng.tensor_tensor(
-                out=z_b[b, i][:],
-                in0=z_t[b, i][:],
+                out=z_b[i][:],
+                in0=z_t[i][:],
                 in1=g_sb[:].unsqueeze(1).to_broadcast([P, P, 4]),
                 op=ALU.mult,
             )
 
-        def z_quant(b, i):
-            if i == 0:
-                z_codes[b] = keep.tile([P, T], I32, name="z_codes", tag="z_codes", align_bytes=64)
-                z_scales[b] = keep.tile([P, T], U8, name="z_scales", tag="z_scales", align_bytes=64)
-            cols = slice(P * i, P * (i + 1))
+        def z_quant(i):
+            b, t_i = divmod(i, NT)
+            cols = slice(P * t_i, P * (t_i + 1))
             nc.vector.quantize_mx(
                 out=z_codes[b][:, cols].bitcast(FP8X4),
                 scales=z_scales[b][:, cols],
-                in_=z_b[b, i][:].rearrange("m p t -> m (p t)"),
+                in_=z_b[i][:].rearrange("m p t -> m (p t)"),
             )
 
-        NU = B * NL
-        s_ps, p_ps, neg, dsum, rinv, ex, vt, wt = {}, {}, {}, {}, {}, {}, {}, {}
-        groups = [list(range(4 * q, 4 * q + 4)) for q in range(NU // 4 - 1)]
-        groups += [[NU - 4, NU - 3], [NU - 2], [NU - 1]]
-        group_of = {}
-        for gi in range(len(groups)):
-            for u in groups[gi]:
-                group_of[u] = gi
-        y32, y16 = {}, {}
-        o_scales = const.tile([P, B * L], U8, name="o_scales", align_bytes=64)
+        s_ps, p_ps, t_ps, neg, dsum, rinv, ex, vt, y16 = {}, {}, {}, {}, {}, {}, {}, {}, {}
+        y32, o_codes = {}, {}
+        for q in range(NU // 2):
+            y32[q] = const.tile([P, 4, 2 * P], F32, name="y32_%d" % q)
+        for q in range(NU // 4):
+            o_codes[q] = const.tile([P, 4 * P], I32, name="o_codes_%d" % q, align_bytes=64)
+        o_scales = {}
+        for b in range(B):
+            o_scales[b] = const.tile([P, L], U8, name="o_scales_%d" % b, align_bytes=64)
 
         def s_mm(u):
             b, j = divmod(u, NL)
             cols = slice(P * j, P * (j + 1))
-            s_ps[u] = psum.tile([P, T], F32, name="s_ps", tag="s", bufs=PB["s"])
+            s_ps[u] = psum.tile([P, T], F32, name="s_ps", tag="s", bufs=BANKS["s"])
             nc.tensor.matmul_mx(
                 out=s_ps[u][:],
                 lhsT=u_sb[:, cols].bitcast(FP8X4),
@@ -182,7 +188,7 @@ def tile_laatlabelwisetokenevidence_x2_kernel(
         def p_mm(u):
             b, j = divmod(u, NL)
             cols = slice(P * j, P * (j + 1))
-            p_ps[u] = psum.tile([P, T], F32, name="p_ps", tag="p", bufs=PB["p"])
+            p_ps[u] = psum.tile([P, T], F32, name="p_ps", tag="p", bufs=BANKS["p"])
             nc.tensor.matmul_mx(
                 out=p_ps[u][:],
                 lhsT=b_sb[:, cols].bitcast(FP8X4),
@@ -193,137 +199,147 @@ def tile_laatlabelwisetokenevidence_x2_kernel(
                 stop=True,
             )
 
-        def vmax(u):
+        def row_max(u):
             neg[u] = stats.tile([P, 1], F32, name="neg", tag="neg")
             nc.vector.tensor_reduce(out=neg[u][:], in_=s_ps[u][:], axis=AX.X, op=ALU.max, negate=True)
 
-        def sexp(u):
+        def row_exp(u):
             ex[u] = stage.tile([P, T], F32, name="ex", tag="ex")
             dsum[u] = stats.tile([P, 1], F32, name="dsum", tag="dsum")
-            nc.scalar.activation(
-                out=ex[u][:], in_=s_ps[u][:], func=ACT.Exp, bias=neg[u][:], accum_out=dsum[u][:]
-            )
+            nc.scalar.activation(out=ex[u][:], in_=s_ps[u][:], func=ACT.Exp, bias=neg[u][:], accum_out=dsum[u][:])
 
-        def vmul(u):
+        def invert(u):
             rinv[u] = stats.tile([P, 1], F32, name="rinv", tag="rinv")
             nc.vector.reciprocal(out=rinv[u][:], in_=dsum[u][:])
+
+        def product(u):
             vt[u] = stage.tile([P, T], F32, name="vt", tag="vt")
             nc.vector.scalar_tensor_tensor(
-                out=vt[u][:], in0=p_ps[u][:], scalar=float(T), in1=ex[u][:], op0=ALU.mult, op1=ALU.mult
-            )
-
-        def affine(u):
-            wt[u] = stage.tile([P, T], F32, name="wt", tag="wt")
-            j = u % NL
-            nc.gpsimd.tensor_scalar(
-                out=wt[u][:], in0=vt[u][:], scalar1=rinv[u][:], scalar2=c_sb[:, j : j + 1], op0=ALU.mult, op1=ALU.add
+                out=vt[u][:], in0=p_ps[u][:], scalar=rinv[u][:], in1=ex[u][:], op0=ALU.mult, op1=ALU.mult
             )
 
         def turn(u):
-            gi = group_of[u]
-            n = len(groups[gi])
-            k = u - groups[gi][0]
-            if k == 0:
-                y32[gi] = stage.tile([P, 4, n * P], F32, name="y32", tag="y32")
-                y16[gi] = stage.tile([P, n * P, 4], BF16, name="y16", tag="y16", align_bytes=64)
-            bank = psum.tile([P, 4, P], F32, name="tp", tag="t", bufs=PB["t"])
-            for t in range(4):
-                nc.tensor.transpose(bank[:, t, :], wt[u][:, P * t : P * (t + 1)], ident[:])
-            nc.scalar.copy(out=y32[gi][:, :, P * k : P * (k + 1)], in_=bank[:])
-
-        def round_out(u):
-            gi = group_of[u]
-            k = u - groups[gi][0]
-            cols = slice(P * k, P * (k + 1))
-            nc.vector.tensor_copy(out=y16[gi][:, cols, :], in_=y32[gi][:, :, cols].rearrange("p t l -> p l t"))
-
-        def store_y(gi):
-            u0, n = groups[gi][0], len(groups[gi])
-            b, j = divmod(u0, NL)
-            dst = out_0[b].rearrange("(p t) l -> p t l", t=4)
-            nc.sync.dma_start(out=dst[:, :, P * j : P * (j + n)], in_=y32[gi][:])
-
-        def quant_out(gi):
-            u0, n = groups[gi][0], len(groups[gi])
-            m0, m1 = P * u0, P * (u0 + n)
-            o_codes = stage.tile([P, n * P], I32, name="o_codes", tag="o_codes", align_bytes=64)
-            nc.vector.quantize_mx(
-                out=o_codes[:].bitcast(FP8X4),
-                scales=o_scales[:, m0:m1],
-                in_=y16[gi][:].rearrange("p l t -> p (l t)"),
+            j = u % NL
+            t_ps[u] = psum.tile([P, 4, P], F32, name="t_ps", tag="t", bufs=BANKS["t"])
+            nc.tensor.matmul(
+                out=t_ps[u][:],
+                lhsT=spread[:],
+                rhs=c_row[:, P * j : P * (j + 1)].unsqueeze(1).to_broadcast([P, 4, P]),
+                start=True,
+                stop=False,
             )
-            nc.sync.dma_start(out=out_words[:, 4 * m0 : 4 * m1].bitcast(I32), in_=o_codes[:])
-            u1 = u0 + n
-            if u1 % NL == 0:
-                m0 = P * (u1 - NL)
-                for q in range(4):
+            for t in range(4):
+                nc.tensor.matmul(
+                    out=t_ps[u][:, t, :],
+                    lhsT=vt[u][:, P * t : P * (t + 1)],
+                    rhs=ident[:],
+                    is_transpose=True,
+                    start=False,
+                    stop=(t == 3),
+                )
+
+        def y_copy(u):
+            q, k = divmod(u, 2)
+            nc.scalar.activation(out=y32[q][:, :, P * k : P * (k + 1)], in_=t_ps[u][:], func=ACT.Copy, scale=float(T))
+            if k == 1:
+                b, j = divmod(u - 1, NL)
+                dst = out_0[b].rearrange("(p t) l -> p t l", t=4)
+                nc.sync.dma_start(out=dst[:, :, P * j : P * (j + 2)], in_=y32[q][:])
+
+        def y_round(u, eng):
+            q, k = divmod(u, 2)
+            y16[u] = bf16_tile(eng)
+            src = y32[q][:, :, P * k : P * (k + 1)].rearrange("p t l -> p l t")
+            if eng is nc.gpsimd:
+                eng.tensor_scalar(out=y16[u][:], in0=src, scalar1=1.0, scalar2=1.0, op0=ALU.mult, op1=ALU.mult)
+            else:
+                eng.tensor_copy(out=y16[u][:], in_=src)
+
+        def y_quant(u):
+            q, k = divmod(u, 4)
+            b, j = divmod(u, NL)
+            nc.vector.quantize_mx(
+                out=o_codes[q][:, P * k : P * (k + 1)].bitcast(FP8X4),
+                scales=o_scales[b][:, P * j : P * (j + 1)],
+                in_=y16[u][:].rearrange("p l t -> p (l t)"),
+            )
+            if k == 3:
+                m0 = 4 * P * q
+                nc.sync.dma_start(out=out_words[:, 4 * m0 : 4 * (m0 + 4 * P)].bitcast(I32), in_=o_codes[q][:])
+            if j == NL - 1:
+                for r in range(4):
                     nc.sync.dma_start(
-                        out=out_2[0, 4 * q : 4 * q + 4, m0:m1].bitcast(I32),
-                        in_=o_scales[32 * q : 32 * q + 4, m0:m1].bitcast(I32),
+                        out=out_2[0, 4 * r : 4 * r + 4, L * b : L * (b + 1)].bitcast(I32),
+                        in_=o_scales[b][32 * r : 32 * r + 4, :].bitcast(I32),
                     )
 
-        h_turn(0, 0, "t")
-        h_turn(0, 1, "t")
+        h_turn(0, "t")
+        h_turn(1, "t")
+        h_copy(0)
+        h_copy(1)
         prep_w()
-        h_quant(0, 0)
-        z_mm(0, 0, "z")
-        h_quant(0, 1)
-        z_mm(0, 1, "s")
-        h_turn(0, 2, "t")
-        z_gain(0, 0, nc.vector)
-        h_quant(0, 2)
-        z_mm(0, 2, "s")
-        z_quant(0, 0)
-        h_turn(0, 3, "t")
-        z_gain(0, 1, nc.vector)
-        h_quant(0, 3)
-        z_mm(0, 3, "s")
-        z_quant(0, 1)
-        prep_c()
-        z_gain(0, 2, nc.vector)
-        z_gain(0, 3, nc.vector)
-        z_quant(0, 2)
-        z_quant(0, 3)
-        s_mm(0)
-        s_mm(1)
-        p_mm(0)
-        vmax(0)
-        sexp(0)
+        h_quant(0)
+        z_mm(0, "s")
+        z_mm(1, "s")
+        h_quant(1)
+        z_mm(2, "s")
+        z_mm(3, "p")
+        for i in range(NT):
+            z_tanh(i)
+            z_gain(i, nc.vector)
+            if i > 0:
+                z_quant(i - 1)
+        z_quant(NT - 1)
 
-        for k in range(NU + 5):
-            b, j = divmod(k, NL)
-            nb = b + 1
-            if k + 1 < NU:
-                vmax(k + 1)
-            if 0 <= k - 2 < NU:
-                turn(k - 2)
-            if k + 2 < NU:
-                s_mm(k + 2)
-            if k + 1 < NU:
+        def unit(u):
+            return 0 <= u < NU
+
+        def half_at(k, lag):
+            hh, r = divmod(k - lag + 14, 4)
+            return hh if r == 0 and 2 <= hh < 2 * B else None
+
+        def tile_at(k, lag):
+            for i in range(2):
+                hh = half_at(k, lag + i)
+                if hh is not None:
+                    return 2 * hh + i
+            return None
+
+        for k in range(-6, NU + 4):
+            gain_now, gain_before = tile_at(k, 4), tile_at(k - 1, 4)
+            if half_at(k, 1) is not None:
+                h_copy(half_at(k, 1))
+            if tile_at(k, 3) is not None:
+                z_tanh(tile_at(k, 3))
+            if unit(k + 1):
+                row_exp(k + 1)
+            if unit(k - 2):
+                y_copy(k - 2)
+            if unit(k + 1):
                 p_mm(k + 1)
-            if nb < B:
-                if 0 <= j - 1 < 4:
-                    z_mm(nb, j - 1, "z")
-                if j < 4:
-                    h_turn(nb, j, "t")
-                if 0 <= j - 2 < 4:
-                    z_gain(nb, j - 2, nc.gpsimd)
-            if k + 1 < NU:
-                sexp(k + 1)
-            if k < NU:
-                vmul(k)
-                affine(k)
-            if 0 <= k - 3 < NU:
-                round_out(k - 3)
-                gi = group_of[k - 3]
-                if groups[gi][-1] == k - 3:
-                    store_y(gi)
-            if nb < B:
-                if j < 4:
-                    h_quant(nb, j)
-                if 0 <= j - 2 < 4:
-                    z_quant(nb, j - 2)
-            if 0 <= k - 4 < NU:
-                gi = group_of[k - 4]
-                if groups[gi][-1] == k - 4:
-                    quant_out(gi)
+            if unit(k + 3):
+                s_mm(k + 3)
+            if tile_at(k, 2) is not None:
+                z_mm(tile_at(k, 2), "z")
+            if unit(k - 1):
+                turn(k - 1)
+            if half_at(k, 0) is not None:
+                h_turn(half_at(k, 0), "z")
+            if gain_now is not None:
+                z_gain(gain_now, nc.gpsimd)
+            elif unit(k - 3):
+                y_round(k - 3, nc.gpsimd)
+            if unit(k):
+                invert(k)
+            if unit(k + 2):
+                row_max(k + 2)
+            if unit(k):
+                product(k)
+            if gain_now is not None and unit(k - 3):
+                y_round(k - 3, nc.vector)
+            if half_at(k, 1) is not None:
+                h_quant(half_at(k, 1))
+            if unit(k - 4):
+                y_quant(k - 4)
+            if gain_before is not None:
+                z_quant(gain_before)

@@ -69,15 +69,16 @@ def tile_laatlabelwisetokenevidence_x2_kernel(
         load_h(0)
         nc.sync.dma_start(out=w_raw[:], in_=w_words[0].rearrange("p n t -> p (n t)").bitcast(I32))
         load_h(1)
-        load_scales(nc.scalar, ws_raw, w_scales)
-        nc.scalar.dma_start(out=g_bf[:], in_=g.rearrange("(p t) -> p t", t=4))
+        load_scales(nc.sync, ws_raw, w_scales)
+        nc.sync.dma_start(out=g_bf[:], in_=g.rearrange("(p t) -> p t", t=4))
         load_h(2)
+        load_h(3)
         nc.sync.dma_start(out=u_sb[:], in_=u_words[0].rearrange("p n t -> p (n t)").bitcast(I32))
         load_scales(nc.sync, us_sb, u_scales)
         nc.sync.dma_start(out=b_sb[:], in_=beta_words[0].rearrange("p n t -> p (n t)").bitcast(I32))
         load_scales(nc.sync, bs_sb, beta_scales)
         nc.sync.dma_start(out=c_row[0:1, :], in_=c.rearrange("(o l) -> o l", o=1))
-        for hh in range(3, 2 * B):
+        for hh in range(4, 2 * B):
             load_h(hh)
 
         nc.scalar.activation(out=warm[:], in_=warm[:], func=ACT.Exp)
@@ -88,8 +89,8 @@ def tile_laatlabelwisetokenevidence_x2_kernel(
         g_sb = const.tile([P, 4], F32, name="g_sb")
 
         def prep_w():
-            nc.vector.tensor_copy(out=w_sb[:], in_=w_raw[:].rearrange("p (m t) -> p t m", t=4))
             nc.vector.tensor_copy(out=ws_sb[:], in_=ws_raw[:].rearrange("p (m t) -> p t m", t=4))
+            nc.vector.tensor_copy(out=w_sb[:], in_=w_raw[:].rearrange("p (m t) -> p t m", t=4))
             nc.vector.tensor_copy(out=g_sb[:], in_=g_bf[:])
 
         h_codes, h_scales, z_codes, z_scales = {}, {}, {}, {}
@@ -100,24 +101,24 @@ def tile_laatlabelwisetokenevidence_x2_kernel(
             z_scales[b] = const.tile([P, T], U8, name="z_scales_%d" % b, align_bytes=64)
         h_bank, h_il, z_bank, z_t, z_b = {}, {}, {}, {}, {}
 
-        def h_turn(hh, tag):
-            words = h_sb[hh][:].bitcast(F32)
-            h_bank[hh] = psum.tile([P, 2, 2, P], F32, name="h_bank", tag=tag, bufs=BANKS[tag])
-            for i in range(2):
+        def h_turn(i, n, tag):
+            words = h_sb[i // 2][:].bitcast(F32)
+            h_bank[i] = psum.tile([P, n, 2, P], F32, name="h_bank", tag=tag, bufs=BANKS[tag])
+            for d in range(n):
                 for e in range(2):
-                    nc.tensor.transpose(h_bank[hh][:, i, e, :], words[:, i, e : D // 2 : 2], ident[:])
+                    nc.tensor.transpose(h_bank[i][:, d, e, :], words[:, i % 2 + d, e : D // 2 : 2], ident[:])
 
-        def h_copy(hh):
-            h_il[hh] = stage.tile([P, 2, P, 4], BF16, name="h_il", tag="h_il", bufs=2, align_bytes=64)
-            nc.scalar.copy(out=h_il[hh][:].bitcast(F32), in_=h_bank[hh][:].rearrange("m i e p -> m i p e"))
+        def h_copy(i, n):
+            h_il[i] = stage.tile([P, n, P, 4], BF16, name="h_il", tag="h_il", align_bytes=64)
+            nc.scalar.copy(out=h_il[i][:].bitcast(F32), in_=h_bank[i][:].rearrange("m i e p -> m i p e"))
 
-        def h_quant(hh):
-            b, hf = divmod(hh, 2)
-            cols = slice(2 * P * hf, 2 * P * (hf + 1))
+        def h_quant(i, n):
+            b, t_i = divmod(i, NT)
+            cols = slice(P * t_i, P * (t_i + n))
             nc.vector.quantize_mx(
                 out=h_codes[b][:, cols].bitcast(FP8X4),
                 scales=h_scales[b][:, cols],
-                in_=h_il[hh][:].rearrange("m i p t -> m (i p t)"),
+                in_=h_il[i][:].rearrange("m i p t -> m (i p t)"),
             )
 
         def z_mm(i, tag):
@@ -139,16 +140,14 @@ def tile_laatlabelwisetokenevidence_x2_kernel(
             z_t[i] = stage.tile([P, P, 4], F32, name="z_t", tag="z_t")
             nc.scalar.activation(out=z_t[i][:], in_=z_bank[i][:].rearrange("m t n -> m n t"), func=ACT.Tanh)
 
-        def bf16_tile(eng):
-            tag = "by_gpsimd" if eng is nc.gpsimd else "by_vector"
-            return stage.tile([P, P, 4], BF16, name=tag, tag=tag, bufs=2 if eng is nc.gpsimd else 4, align_bytes=64)
-
-        def z_gain(i, eng):
-            z_b[i] = bf16_tile(eng)
+        def z_gain(i, eng, lo, hi):
+            if i not in z_b:
+                tag = "z_b_head" if i < NT else "z_b"
+                z_b[i] = stage.tile([P, P, 4], BF16, name=tag, tag=tag, bufs=NT if i < NT else 2, align_bytes=64)
             eng.tensor_tensor(
-                out=z_b[i][:],
-                in0=z_t[i][:],
-                in1=g_sb[:].unsqueeze(1).to_broadcast([P, P, 4]),
+                out=z_b[i][:, lo:hi, :],
+                in0=z_t[i][:, lo:hi, :],
+                in1=g_sb[:].unsqueeze(1).to_broadcast([P, hi - lo, 4]),
                 op=ALU.mult,
             )
 
@@ -241,105 +240,152 @@ def tile_laatlabelwisetokenevidence_x2_kernel(
         def y_copy(u):
             q, k = divmod(u, 2)
             nc.scalar.activation(out=y32[q][:, :, P * k : P * (k + 1)], in_=t_ps[u][:], func=ACT.Copy, scale=float(T))
-            if k == 1:
-                b, j = divmod(u - 1, NL)
-                dst = out_0[b].rearrange("(p t) l -> p t l", t=4)
-                nc.sync.dma_start(out=dst[:, :, P * j : P * (j + 2)], in_=y32[q][:])
 
-        def y_round(u, eng):
+        def y_store(u, n):
             q, k = divmod(u, 2)
-            y16[u] = bf16_tile(eng)
-            src = y32[q][:, :, P * k : P * (k + 1)].rearrange("p t l -> p l t")
+            b, j = divmod(u, NL)
+            dst = out_0[b].rearrange("(p t) l -> p t l", t=4)
+            nc.sync.dma_start(out=dst[:, :, P * j : P * (j + n)], in_=y32[q][:, :, P * k : P * (k + n)])
+
+        def y_round(u, n, eng):
+            q, k = divmod(u, 2)
+            src = y32[q][:, :, P * k : P * (k + n)].rearrange("p t l -> p l t")
             if eng is nc.gpsimd:
+                y16[u] = stage.tile([P, n * P, 4], BF16, name="y16", tag="y16", bufs=2, align_bytes=64)
                 eng.tensor_scalar(out=y16[u][:], in0=src, scalar1=1.0, scalar2=1.0, op0=ALU.mult, op1=ALU.mult)
             else:
+                y16[u] = stage.tile([P, n * P, 4], BF16, name="y16_last", tag="y16_last", bufs=2, align_bytes=64)
                 eng.tensor_copy(out=y16[u][:], in_=src)
 
-        def y_quant(u):
+        def y_quant(u, n):
             q, k = divmod(u, 4)
             b, j = divmod(u, NL)
             nc.vector.quantize_mx(
-                out=o_codes[q][:, P * k : P * (k + 1)].bitcast(FP8X4),
-                scales=o_scales[b][:, P * j : P * (j + 1)],
+                out=o_codes[q][:, P * k : P * (k + n)].bitcast(FP8X4),
+                scales=o_scales[b][:, P * j : P * (j + n)],
                 in_=y16[u][:].rearrange("p l t -> p (l t)"),
             )
-            if k == 3:
-                m0 = 4 * P * q
-                nc.sync.dma_start(out=out_words[:, 4 * m0 : 4 * (m0 + 4 * P)].bitcast(I32), in_=o_codes[q][:])
-            if j == NL - 1:
-                for r in range(4):
-                    nc.sync.dma_start(
-                        out=out_2[0, 4 * r : 4 * r + 4, L * b : L * (b + 1)].bitcast(I32),
-                        in_=o_scales[b][32 * r : 32 * r + 4, :].bitcast(I32),
-                    )
 
-        h_turn(0, "t")
-        h_turn(1, "t")
-        h_copy(0)
-        h_copy(1)
+        def codes_store(u, n):
+            q, k = divmod(u, 4)
+            nc.sync.dma_start(
+                out=out_words[:, 4 * P * u : 4 * P * (u + n)].bitcast(I32), in_=o_codes[q][:, P * k : P * (k + n)]
+            )
+
+        def scales_store(b, engines):
+            for r in range(4):
+                engines[r].dma_start(
+                    out=out_2[0, 4 * r : 4 * r + 4, L * b : L * (b + 1)].bitcast(I32),
+                    in_=o_scales[b][32 * r : 32 * r + 4, :].bitcast(I32),
+                )
+
+        GP = P // 2
+        h_turn(0, 1, "t")
+        h_turn(1, 1, "t")
+        h_turn(2, 1, "p")
+        h_turn(3, 1, "p")
         prep_w()
-        h_quant(0)
-        z_mm(0, "s")
-        z_mm(1, "s")
-        h_quant(1)
-        z_mm(2, "s")
-        z_mm(3, "p")
+        for i in range(NT):
+            h_copy(i, 1)
+            h_quant(i, 1)
+            z_mm(i, "s" if i < 3 else "z")
+        h_turn(4, 2, "t")
+        h_turn(6, 2, "t")
         for i in range(NT):
             z_tanh(i)
-            z_gain(i, nc.vector)
+        h_copy(4, 2)
+        h_copy(6, 2)
+        for i in range(NT):
+            z_gain(i, nc.vector, 0, P)
+            if i == NT - 1:
+                h_quant(4, 2)
             if i > 0:
                 z_quant(i - 1)
         z_quant(NT - 1)
+        h_quant(6, 2)
+        z_mm(4, "t")
+        z_tanh(4)
+        s_mm(0)
+        z_mm(5, "t")
+        z_tanh(5)
+        s_mm(1)
+        s_mm(2)
+        for u in range(3):
+            row_max(u)
+        p_mm(0)
+        z_mm(6, "z")
+        row_exp(0)
+        z_tanh(6)
+        h_turn(8, 2, "t")
 
         def unit(u):
             return 0 <= u < NU
 
-        def half_at(k, lag):
-            hh, r = divmod(k - lag + 14, 4)
-            return hh if r == 0 and 2 <= hh < 2 * B else None
+        def tile(i):
+            return NT + 2 <= i < B * NT
 
-        def tile_at(k, lag):
-            for i in range(2):
-                hh = half_at(k, lag + i)
-                if hh is not None:
-                    return 2 * hh + i
-            return None
-
-        for k in range(-6, NU + 4):
-            gain_now, gain_before = tile_at(k, 4), tile_at(k - 1, 4)
-            if half_at(k, 1) is not None:
-                h_copy(half_at(k, 1))
-            if tile_at(k, 3) is not None:
-                z_tanh(tile_at(k, 3))
+        LAST = NU - 4
+        for k in range(NU + 5):
+            pair, second = divmod(k, 2)
+            z_i = pair + 7
+            h_i = pair + 9
+            h_turn_now = second and h_i % 2 == 0 and 2 * NT <= h_i < B * NT
+            h_copy_now = (h_i - 1) % 2 == 0 and 2 * NT <= h_i - 1 < B * NT
             if unit(k + 1):
                 row_exp(k + 1)
+            if h_copy_now and not second:
+                h_copy(h_i - 1, 2)
+            if tile(z_i) and second:
+                z_tanh(z_i)
             if unit(k - 2):
                 y_copy(k - 2)
+                if k - 2 >= NU - 2:
+                    y_store(k - 2, 1)
+                elif second:
+                    y_store(k - 3, 2)
             if unit(k + 1):
                 p_mm(k + 1)
             if unit(k + 3):
                 s_mm(k + 3)
-            if tile_at(k, 2) is not None:
-                z_mm(tile_at(k, 2), "z")
             if unit(k - 1):
                 turn(k - 1)
-            if half_at(k, 0) is not None:
-                h_turn(half_at(k, 0), "z")
-            if gain_now is not None:
-                z_gain(gain_now, nc.gpsimd)
-            elif unit(k - 3):
-                y_round(k - 3, nc.gpsimd)
+            if tile(z_i) and not second:
+                z_mm(z_i, "z")
+            if h_turn_now:
+                h_turn(h_i, 2, "z")
+            if not second:
+                if 0 <= k - 4 < LAST:
+                    y_round(k - 4, 2, nc.gpsimd)
+                if pair < 2:
+                    z_gain(NT + 2 * pair, nc.gpsimd, 0, P)
+                    z_gain(NT + 2 * pair + 1, nc.gpsimd, 0, P if pair == 0 else GP)
+                elif tile(z_i - 1):
+                    z_gain(z_i - 1, nc.gpsimd, 0, GP)
             if unit(k):
                 invert(k)
-            if unit(k + 2):
+            if unit(k + 2) and k > 0:
                 row_max(k + 2)
             if unit(k):
                 product(k)
-            if gain_now is not None and unit(k - 3):
-                y_round(k - 3, nc.vector)
-            if half_at(k, 1) is not None:
-                h_quant(half_at(k, 1))
-            if unit(k - 4):
-                y_quant(k - 4)
-            if gain_before is not None:
-                z_quant(gain_before)
+            if second:
+                if 0 <= k - 7 < LAST:
+                    y_quant(k - 7, 2)
+                    if (k - 7) % 4 == 2:
+                        codes_store(k - 9, 4)
+                    if (k - 7) % NL == NL - 2:
+                        scales_store((k - 7) // NL, [nc.sync] * 4)
+                if 0 <= pair < 2:
+                    z_quant(NT + 2 * pair)
+                    z_quant(NT + 2 * pair + 1)
+                elif tile(z_i - 1):
+                    z_quant(z_i - 1)
+                if h_copy_now:
+                    h_quant(h_i - 1, 2)
+                if tile(z_i):
+                    z_gain(z_i, nc.vector, GP, P)
+            if LAST <= k - 3 < NU:
+                y_round(k - 3, 1, nc.vector)
+            if LAST <= k - 4 < NU:
+                y_quant(k - 4, 1)
+        codes_store(LAST, 4)
+        scales_store(B - 1, [nc.scalar, nc.sync, nc.scalar, nc.sync])

@@ -45,8 +45,6 @@ def tile_laatlabelwisetokenevidence_x2_kernel(
             src = h[b].rearrange("(p t) d -> p t d", t=NT)
             nc.sync.dma_start(out=h_sb[hh][:], in_=src[:, 2 * hf : 2 * hf + 2, :])
 
-        warm = const.tile([P, 1], F32, name="warm")
-        nc.vector.memset(warm[:], 0.0)
         w_raw = const.tile([P, A], I32, name="w_raw", align_bytes=64)
         ws_raw = const.tile([P, A], U8, name="ws_raw", align_bytes=64)
         u_sb = const.tile([P, L], I32, name="u_sb", align_bytes=64)
@@ -81,7 +79,6 @@ def tile_laatlabelwisetokenevidence_x2_kernel(
         for hh in range(4, 2 * B):
             load_h(hh)
 
-        nc.scalar.activation(out=warm[:], in_=warm[:], func=ACT.Exp)
         ident = const.tile([P, P], F32, name="ident", align_bytes=64)
         make_identity(nc, ident[:])
         w_sb = const.tile([P, 4, P], I32, name="w_sb", align_bytes=64)
@@ -160,7 +157,9 @@ def tile_laatlabelwisetokenevidence_x2_kernel(
                 in_=z_b[i][:].rearrange("m p t -> m (p t)"),
             )
 
-        s_ps, p_ps, t_ps, neg, dsum, rinv, ex, vt, y16 = {}, {}, {}, {}, {}, {}, {}, {}, {}
+        s_ps, p_ps, t_ps, neg, ex, vt, y16 = {}, {}, {}, {}, {}, {}, {}
+        dsum = const.tile([P, NU], F32, name="dsum")
+        rinv = const.tile([P, NU], F32, name="rinv")
         y32, o_codes = {}, {}
         for q in range(NU // 2):
             y32[q] = const.tile([P, 4, 2 * P], F32, name="y32_%d" % q)
@@ -184,10 +183,10 @@ def tile_laatlabelwisetokenevidence_x2_kernel(
                 stop=True,
             )
 
-        def p_mm(u):
+        def p_mm(u, tag="p"):
             b, j = divmod(u, NL)
             cols = slice(P * j, P * (j + 1))
-            p_ps[u] = psum.tile([P, T], F32, name="p_ps", tag="p", bufs=BANKS["p"])
+            p_ps[u] = psum.tile([P, T], F32, name="p_ps", tag=tag, bufs=BANKS[tag])
             nc.tensor.matmul_mx(
                 out=p_ps[u][:],
                 lhsT=b_sb[:, cols].bitcast(FP8X4),
@@ -203,23 +202,23 @@ def tile_laatlabelwisetokenevidence_x2_kernel(
             nc.vector.tensor_reduce(out=neg[u][:], in_=s_ps[u][:], axis=AX.X, op=ALU.max, negate=True)
 
         def row_exp(u):
-            ex[u] = stage.tile([P, T], F32, name="ex", tag="ex")
-            dsum[u] = stats.tile([P, 1], F32, name="dsum", tag="dsum")
-            nc.scalar.activation(out=ex[u][:], in_=s_ps[u][:], func=ACT.Exp, bias=neg[u][:], accum_out=dsum[u][:])
+            ex[u] = stage.tile([P, T], F32, name="ex", tag="ex", bufs=5)
+            nc.scalar.activation(
+                out=ex[u][:], in_=s_ps[u][:], func=ACT.Exp, bias=neg[u][:], accum_out=dsum[:, u : u + 1]
+            )
 
-        def invert(u):
-            rinv[u] = stats.tile([P, 1], F32, name="rinv", tag="rinv")
-            nc.vector.reciprocal(out=rinv[u][:], in_=dsum[u][:])
+        def invert(u, n):
+            nc.vector.reciprocal(out=rinv[:, u : u + n], in_=dsum[:, u : u + n])
 
         def product(u):
             vt[u] = stage.tile([P, T], F32, name="vt", tag="vt")
             nc.vector.scalar_tensor_tensor(
-                out=vt[u][:], in0=p_ps[u][:], scalar=rinv[u][:], in1=ex[u][:], op0=ALU.mult, op1=ALU.mult
+                out=vt[u][:], in0=p_ps[u][:], scalar=rinv[:, u : u + 1], in1=ex[u][:], op0=ALU.mult, op1=ALU.mult
             )
 
-        def turn(u):
+        def lay_c(u, tag):
             j = u % NL
-            t_ps[u] = psum.tile([P, 4, P], F32, name="t_ps", tag="t", bufs=BANKS["t"])
+            t_ps[u] = psum.tile([P, 4, P], F32, name="t_ps", tag=tag, bufs=BANKS[tag])
             nc.tensor.matmul(
                 out=t_ps[u][:],
                 lhsT=spread[:],
@@ -227,6 +226,8 @@ def tile_laatlabelwisetokenevidence_x2_kernel(
                 start=True,
                 stop=False,
             )
+
+        def turn(u):
             for t in range(4):
                 nc.tensor.matmul(
                     out=t_ps[u][:, t, :],
@@ -251,10 +252,10 @@ def tile_laatlabelwisetokenevidence_x2_kernel(
             q, k = divmod(u, 2)
             src = y32[q][:, :, P * k : P * (k + n)].rearrange("p t l -> p l t")
             if eng is nc.gpsimd:
-                y16[u] = stage.tile([P, n * P, 4], BF16, name="y16", tag="y16", bufs=2, align_bytes=64)
+                y16[u] = stage.tile([P, n * P, 4], BF16, name="y16", tag="y16", bufs=1, align_bytes=64)
                 eng.tensor_scalar(out=y16[u][:], in0=src, scalar1=1.0, scalar2=1.0, op0=ALU.mult, op1=ALU.mult)
             else:
-                y16[u] = stage.tile([P, n * P, 4], BF16, name="y16_last", tag="y16_last", bufs=2, align_bytes=64)
+                y16[u] = stage.tile([P, n * P, 4], BF16, name="y16_last", tag="y16_last", bufs=3, align_bytes=64)
                 eng.tensor_copy(out=y16[u][:], in_=src)
 
         def y_quant(u, n):
@@ -314,9 +315,12 @@ def tile_laatlabelwisetokenevidence_x2_kernel(
             row_max(u)
         p_mm(0)
         z_mm(6, "z")
-        row_exp(0)
-        z_tanh(6)
         h_turn(8, 2, "t")
+        row_exp(0)
+        s_mm(3)
+        row_exp(1)
+        z_tanh(6)
+        h_copy(8, 2)
 
         def unit(u):
             return 0 <= u < NU
@@ -324,35 +328,51 @@ def tile_laatlabelwisetokenevidence_x2_kernel(
         def tile(i):
             return NT + 2 <= i < B * NT
 
+        def finish_pair(u):
+            y_quant(u, 2)
+            if u % 4 == 2:
+                codes_store(u - 2, 4)
+            if u % NL == NL - 2:
+                scales_store(u // NL, [nc.sync] * 4)
+
         LAST = NU - 4
-        for k in range(NU + 5):
+        for k in range(LAST):
             pair, second = divmod(k, 2)
             z_i = pair + 7
             h_i = pair + 9
             h_turn_now = second and h_i % 2 == 0 and 2 * NT <= h_i < B * NT
             h_copy_now = (h_i - 1) % 2 == 0 and 2 * NT <= h_i - 1 < B * NT
-            if unit(k + 1):
-                row_exp(k + 1)
-            if h_copy_now and not second:
-                h_copy(h_i - 1, 2)
-            if tile(z_i) and second:
-                z_tanh(z_i)
+            if second and unit(k + 2):
+                row_exp(k + 2)
             if unit(k - 2):
                 y_copy(k - 2)
-                if k - 2 >= NU - 2:
-                    y_store(k - 2, 1)
-                elif second:
+                if second:
                     y_store(k - 3, 2)
-            if unit(k + 1):
-                p_mm(k + 1)
-            if unit(k + 3):
-                s_mm(k + 3)
-            if unit(k - 1):
-                turn(k - 1)
-            if tile(z_i) and not second:
-                z_mm(z_i, "z")
-            if h_turn_now:
-                h_turn(h_i, 2, "z")
+            if not second and unit(k + 2):
+                row_exp(k + 2)
+            if not second:
+                if unit(k + 1):
+                    p_mm(k + 1)
+                if unit(k + 4):
+                    s_mm(k + 4)
+                if tile(z_i):
+                    z_mm(z_i, "z")
+                    z_tanh(z_i)
+                for u in (k - 1, k):
+                    if unit(u):
+                        lay_c(u, "t")
+                if unit(k - 1):
+                    turn(k - 1)
+            else:
+                if unit(k - 1):
+                    turn(k - 1)
+                if h_turn_now:
+                    h_turn(h_i, 2, "z")
+                    h_copy(h_i, 2)
+                if unit(k + 4):
+                    s_mm(k + 4)
+                if unit(k + 1):
+                    p_mm(k + 1)
             if not second:
                 if 0 <= k - 4 < LAST:
                     y_round(k - 4, 2, nc.gpsimd)
@@ -361,20 +381,18 @@ def tile_laatlabelwisetokenevidence_x2_kernel(
                     z_gain(NT + 2 * pair + 1, nc.gpsimd, 0, P if pair == 0 else GP)
                 elif tile(z_i - 1):
                     z_gain(z_i - 1, nc.gpsimd, 0, GP)
-            if unit(k):
-                invert(k)
-            if unit(k + 2) and k > 0:
-                row_max(k + 2)
-            if unit(k):
+            if k == 0:
+                invert(0, 1)
+                product(0)
+                invert(1, 1)
+            if unit(k + 3):
+                row_max(k + 3)
+            if unit(k) and k > 0:
                 product(k)
             if second:
-                if 0 <= k - 7 < LAST:
-                    y_quant(k - 7, 2)
-                    if (k - 7) % 4 == 2:
-                        codes_store(k - 9, 4)
-                    if (k - 7) % NL == NL - 2:
-                        scales_store((k - 7) // NL, [nc.sync] * 4)
-                if 0 <= pair < 2:
+                if unit(k - 5):
+                    finish_pair(k - 5)
+                if pair < 2:
                     z_quant(NT + 2 * pair)
                     z_quant(NT + 2 * pair + 1)
                 elif tile(z_i - 1):
@@ -383,9 +401,47 @@ def tile_laatlabelwisetokenevidence_x2_kernel(
                     h_quant(h_i - 1, 2)
                 if tile(z_i):
                     z_gain(z_i, nc.vector, GP, P)
-            if LAST <= k - 3 < NU:
-                y_round(k - 3, 1, nc.vector)
-            if LAST <= k - 4 < NU:
-                y_quant(k - 4, 1)
+                if unit(k + 1):
+                    invert(k + 1, 2)
+
+        y_copy(LAST - 2)
+        row_exp(LAST + 2)
+        p_mm(LAST + 1)
+        lay_c(LAST - 1, "t")
+        turn(LAST - 1)
+        lay_c(LAST, "z")
+        p_mm(LAST + 2, "s")
+        y_round(LAST - 4, 2, nc.gpsimd)
+        row_max(LAST + 3)
+        product(LAST)
+        turn(LAST)
+        row_exp(LAST + 3)
+        y_copy(LAST - 1)
+        y_store(LAST - 2, 2)
+        lay_c(LAST + 1, "p")
+        product(LAST + 1)
+        turn(LAST + 1)
+        p_mm(LAST + 3, "s")
+        lay_c(LAST + 2, "t")
+        invert(LAST + 2, 2)
+        finish_pair(LAST - 4)
+        y_copy(LAST)
+        y_copy(LAST + 1)
+        y_store(LAST, 2)
+        y_round(LAST - 2, 2, nc.gpsimd)
+        for u in (LAST + 2, LAST + 3):
+            product(u)
+            if u == NU - 1:
+                lay_c(u, "s")
+            turn(u)
+            y_copy(u)
+            y_store(u, 1)
+        y_round(LAST, 2, nc.vector)
+        finish_pair(LAST - 2)
+        y_round(LAST + 2, 1, nc.vector)
+        y_quant(LAST, 2)
+        y_round(LAST + 3, 1, nc.vector)
+        y_quant(LAST + 2, 1)
+        y_quant(LAST + 3, 1)
         codes_store(LAST, 4)
         scales_store(B - 1, [nc.scalar, nc.sync, nc.scalar, nc.sync])

@@ -19,6 +19,9 @@ ALU = mybir.AluOpType
 AX = mybir.AxisListType
 
 BANKS = {"s": 3, "p": 2, "t": 2, "z": 1}
+YB = 1
+LAG = 0
+WH = ()
 FLOPS = 2 * B * T * (D * A + A * L + D * L)
 
 
@@ -54,11 +57,19 @@ def tile_laatlabelwisetokenevidence_x2_kernel(
         g_bf = const.tile([P, 4], BF16, name="g_bf")
         c_row = const.tile([P, L], BF16, name="c_row", align_bytes=64)
         spread = const.tile([P, P], BF16, name="spread", align_bytes=64)
+        c_col_bf = const.tile([P, 1], BF16, name="c_col_bf")
+        c_col = const.tile([P, 1], F32, name="c_col")
+        zeros = const.tile([P, P], F32, name="zeros", align_bytes=64)
+        nc.vector.memset(zeros[:], 0.0)
         nc.vector.memset(ws_raw[:].bitcast(I32), 0)
+        nc.vector.memset(c_row[:], 0.0)
         nc.vector.memset(us_sb[:].bitcast(I32), 0)
         nc.vector.memset(bs_sb[:].bitcast(I32), 0)
-        nc.vector.memset(c_row[:], 0.0)
         nc.vector.memset(spread[:], 1.0 / T)
+
+        def warm_up(bank, n):
+            for i in range(n):
+                nc.tensor.matmul(out=bank[:], lhsT=zeros[:], rhs=zeros[:], start=True, stop=True)
 
         def load_scales(eng, dst, src):
             for r in range(4):
@@ -71,13 +82,12 @@ def tile_laatlabelwisetokenevidence_x2_kernel(
         nc.sync.dma_start(out=g_bf[:], in_=g.rearrange("(p t) -> p t", t=4))
         load_h(2)
         load_h(3)
+        load_h(4)
+        load_h(5)
         nc.sync.dma_start(out=u_sb[:], in_=u_words[0].rearrange("p n t -> p (n t)").bitcast(I32))
         load_scales(nc.sync, us_sb, u_scales)
         nc.sync.dma_start(out=b_sb[:], in_=beta_words[0].rearrange("p n t -> p (n t)").bitcast(I32))
         load_scales(nc.sync, bs_sb, beta_scales)
-        nc.sync.dma_start(out=c_row[0:1, :], in_=c.rearrange("(o l) -> o l", o=1))
-        for hh in range(4, 2 * B):
-            load_h(hh)
 
         ident = const.tile([P, P], F32, name="ident", align_bytes=64)
         make_identity(nc, ident[:])
@@ -106,7 +116,7 @@ def tile_laatlabelwisetokenevidence_x2_kernel(
                     nc.tensor.transpose(h_bank[i][:, d, e, :], words[:, i % 2 + d, e : D // 2 : 2], ident[:])
 
         def h_copy(i, n):
-            h_il[i] = stage.tile([P, n, P, 4], BF16, name="h_il", tag="h_il", align_bytes=64)
+            h_il[i] = stage.tile([P, n, P, 4], BF16, name="h_il", tag="h_il", bufs=6, align_bytes=64)
             nc.scalar.copy(out=h_il[i][:].bitcast(F32), in_=h_bank[i][:].rearrange("m i e p -> m i p e"))
 
         def h_quant(i, n):
@@ -139,8 +149,8 @@ def tile_laatlabelwisetokenevidence_x2_kernel(
 
         def z_gain(i, eng, lo, hi):
             if i not in z_b:
-                tag = "z_b_head" if i < NT else "z_b"
-                z_b[i] = stage.tile([P, P, 4], BF16, name=tag, tag=tag, bufs=NT if i < NT else 2, align_bytes=64)
+                tag, bufs = ("y16", YB) if i in (NT, NT + 2) else ("z_b", NT)
+                z_b[i] = stage.tile([P, P, 4], BF16, name=tag, tag=tag, bufs=bufs, align_bytes=64)
             eng.tensor_tensor(
                 out=z_b[i][:, lo:hi, :],
                 in0=z_t[i][:, lo:hi, :],
@@ -160,14 +170,30 @@ def tile_laatlabelwisetokenevidence_x2_kernel(
         s_ps, p_ps, t_ps, neg, ex, vt, y16 = {}, {}, {}, {}, {}, {}, {}
         dsum = const.tile([P, NU], F32, name="dsum")
         rinv = const.tile([P, NU], F32, name="rinv")
-        y32, o_codes = {}, {}
-        for q in range(NU // 2):
-            y32[q] = const.tile([P, 4, 2 * P], F32, name="y32_%d" % q)
-        for q in range(NU // 4):
-            o_codes[q] = const.tile([P, 4 * P], I32, name="o_codes_%d" % q, align_bytes=64)
-        o_scales = {}
-        for b in range(B):
-            o_scales[b] = const.tile([P, L], U8, name="o_scales_%d" % b, align_bytes=64)
+        o_codes = const.tile([P, NU * P], I32, name="o_codes", align_bytes=64)
+        o_scales = const.tile([P, NU * P], U8, name="o_scales", align_bytes=64)
+
+        def whole(pair):
+            return pair in WH
+
+        groups, round_at = [], {}
+        done = 0
+        for pair in range(2, NU // 2 - 1):
+            if pair + 6 < B * NT:
+                n = 1 if whole(pair) else 2
+            else:
+                n = min(3, 2 * pair - 2 - done)
+            round_at[pair] = len(groups)
+            groups.append((done, n))
+            done = done + n
+        groups.extend([(done, 2), (done + 2, 2), (done + 4, 1), (done + 5, 1)])
+        assert done + 6 == NU
+        group_of, y32 = {}, {}
+        for gi in range(len(groups)):
+            u0, n = groups[gi]
+            y32[gi] = const.tile([P, 4, n * P], F32, name="y32_%d" % gi)
+            for u in range(u0, u0 + n):
+                group_of[u] = gi
 
         def s_mm(u):
             b, j = divmod(u, NL)
@@ -219,6 +245,17 @@ def tile_laatlabelwisetokenevidence_x2_kernel(
         def lay_c(u, tag):
             j = u % NL
             t_ps[u] = psum.tile([P, 4, P], F32, name="t_ps", tag=tag, bufs=BANKS[tag])
+            if j == 0 and u > 0:
+                for t in range(4):
+                    nc.tensor.matmul(
+                        out=t_ps[u][:, t, :],
+                        lhsT=c_col[:].to_broadcast([P, P]),
+                        rhs=ident[:],
+                        is_transpose=True,
+                        start=(t == 0),
+                        stop=False,
+                    )
+                return
             nc.tensor.matmul(
                 out=t_ps[u][:],
                 lhsT=spread[:],
@@ -239,63 +276,77 @@ def tile_laatlabelwisetokenevidence_x2_kernel(
                 )
 
         def y_copy(u):
-            q, k = divmod(u, 2)
-            nc.scalar.activation(out=y32[q][:, :, P * k : P * (k + 1)], in_=t_ps[u][:], func=ACT.Copy, scale=float(T))
+            gi = group_of[u]
+            u0, n = groups[gi]
+            k = u - u0
+            nc.scalar.activation(out=y32[gi][:, :, P * k : P * (k + 1)], in_=t_ps[u][:], func=ACT.Copy, scale=float(T))
+            if k == n - 1:
+                cuts = sorted(set([u0, u0 + n, max(u0, NL * (u // NL))]))
+                for lo, hi in zip(cuts[:-1], cuts[1:]):
+                    b, j = divmod(lo, NL)
+                    dst = out_0[b].rearrange("(p t) l -> p t l", t=4)
+                    nc.sync.dma_start(
+                        out=dst[:, :, P * j : P * (j + hi - lo)], in_=y32[gi][:, :, P * (lo - u0) : P * (hi - u0)]
+                    )
 
-        def y_store(u, n):
-            q, k = divmod(u, 2)
-            b, j = divmod(u, NL)
-            dst = out_0[b].rearrange("(p t) l -> p t l", t=4)
-            nc.sync.dma_start(out=dst[:, :, P * j : P * (j + n)], in_=y32[q][:, :, P * k : P * (k + n)])
-
-        def y_round(u, n, eng):
-            q, k = divmod(u, 2)
-            src = y32[q][:, :, P * k : P * (k + n)].rearrange("p t l -> p l t")
+        def y_round(gi, eng):
+            n = groups[gi][1]
+            src = y32[gi][:].rearrange("p t (c i) -> p c t i", i=4)
             if eng is nc.gpsimd:
-                y16[u] = stage.tile([P, n * P, 4], BF16, name="y16", tag="y16", bufs=1, align_bytes=64)
-                eng.tensor_scalar(out=y16[u][:], in0=src, scalar1=1.0, scalar2=1.0, op0=ALU.mult, op1=ALU.mult)
+                y16[gi] = stage.tile([P, n * P, 4], BF16, name="y16", tag="y16", bufs=YB, align_bytes=64)
+                src = y32[gi][:].rearrange("p t l -> p l t")
+                eng.tensor_scalar(out=y16[gi][:], in0=src, scalar1=1.0, scalar2=1.0, op0=ALU.mult, op1=ALU.mult)
             else:
-                y16[u] = stage.tile([P, n * P, 4], BF16, name="y16_last", tag="y16_last", bufs=3, align_bytes=64)
-                eng.tensor_copy(out=y16[u][:], in_=src)
+                y16[gi] = stage.tile([P, n * P, 4], BF16, name="y16_last", tag="y16_last", bufs=3, align_bytes=64)
+                eng.tensor_copy(out=y16[gi][:].rearrange("p (c i) t -> p c t i", i=4), in_=src)
 
-        def y_quant(u, n):
-            q, k = divmod(u, 4)
-            b, j = divmod(u, NL)
+        def y_quant(gi):
+            u0, n = groups[gi]
+            cols = slice(P * u0, P * (u0 + n))
             nc.vector.quantize_mx(
-                out=o_codes[q][:, P * k : P * (k + n)].bitcast(FP8X4),
-                scales=o_scales[b][:, P * j : P * (j + n)],
-                in_=y16[u][:].rearrange("p l t -> p (l t)"),
+                out=o_codes[:, cols].bitcast(FP8X4),
+                scales=o_scales[:, cols],
+                in_=y16[gi][:].rearrange("p l t -> p (l t)"),
             )
+            for q in range(u0 // 4, (u0 + n) // 4):
+                cols = slice(4 * P * q, 4 * P * (q + 1))
+                nc.sync.dma_start(out=out_words[:].bitcast(I32)[:, cols], in_=o_codes[:, cols])
+            for b in range(u0 // NL, (u0 + n) // NL):
+                for r in range(4):
+                    eng = nc.scalar if b == B - 1 and r % 2 == 0 else nc.sync
+                    eng.dma_start(
+                        out=out_2[0, 4 * r : 4 * r + 4, L * b : L * (b + 1)].bitcast(I32),
+                        in_=o_scales[32 * r : 32 * r + 4, L * b : L * (b + 1)].bitcast(I32),
+                    )
 
-        def codes_store(u, n):
-            q, k = divmod(u, 4)
-            nc.sync.dma_start(
-                out=out_words[:, 4 * P * u : 4 * P * (u + n)].bitcast(I32), in_=o_codes[q][:, P * k : P * (k + n)]
-            )
-
-        def scales_store(b, engines):
-            for r in range(4):
-                engines[r].dma_start(
-                    out=out_2[0, 4 * r : 4 * r + 4, L * b : L * (b + 1)].bitcast(I32),
-                    in_=o_scales[b][32 * r : 32 * r + 4, :].bitcast(I32),
-                )
-
-        GP = P // 2
+        GP = 64
+        early = psum.tile([P, P], F32, name="early", tag="z", bufs=BANKS["z"])
+        warm_up(early, 4)
         h_turn(0, 1, "t")
         h_turn(1, 1, "t")
+        warm_up(early, 1)
+        prep_w()
         h_turn(2, 1, "p")
         h_turn(3, 1, "p")
-        prep_w()
         for i in range(NT):
             h_copy(i, 1)
             h_quant(i, 1)
             z_mm(i, "s" if i < 3 else "z")
-        h_turn(4, 2, "t")
-        h_turn(6, 2, "t")
+        nc.sync.dma_start(out=c_row[0:1, :], in_=c.rearrange("(o l) -> o l", o=1))
+        nc.sync.dma_start(out=c_col_bf[:], in_=c[0:P].rearrange("(p o) -> p o", o=1))
+        for hh in range(6, 2 * B):
+            load_h(hh)
         for i in range(NT):
             z_tanh(i)
+        later = psum.tile([P, P], F32, name="later", tag="s", bufs=BANKS["s"])
+        h_turn(4, 2, "t")
+        h_turn(6, 2, "t")
+        warm_up(later, 2)
         h_copy(4, 2)
         h_copy(6, 2)
+        h_turn(8, 2, "p")
+        warm_up(later, 1)
+        h_copy(8, 2)
         for i in range(NT):
             z_gain(i, nc.vector, 0, P)
             if i == NT - 1:
@@ -304,6 +355,8 @@ def tile_laatlabelwisetokenevidence_x2_kernel(
                 z_quant(i - 1)
         z_quant(NT - 1)
         h_quant(6, 2)
+        h_quant(8, 2)
+        nc.gpsimd.tensor_scalar(out=c_col[:], in0=c_col_bf[:], scalar1=1.0 / T, scalar2=1.0, op0=ALU.mult, op1=ALU.mult)
         z_mm(4, "t")
         z_tanh(4)
         s_mm(0)
@@ -315,12 +368,12 @@ def tile_laatlabelwisetokenevidence_x2_kernel(
             row_max(u)
         p_mm(0)
         z_mm(6, "z")
-        h_turn(8, 2, "t")
+        h_turn(10, 2, "t")
         row_exp(0)
         s_mm(3)
         row_exp(1)
         z_tanh(6)
-        h_copy(8, 2)
+        h_copy(10, 2)
 
         def unit(u):
             return 0 <= u < NU
@@ -328,26 +381,25 @@ def tile_laatlabelwisetokenevidence_x2_kernel(
         def tile(i):
             return NT + 2 <= i < B * NT
 
-        def finish_pair(u):
-            y_quant(u, 2)
-            if u % 4 == 2:
-                codes_store(u - 2, 4)
-            if u % NL == NL - 2:
-                scales_store(u // NL, [nc.sync] * 4)
-
         LAST = NU - 4
         for k in range(LAST):
             pair, second = divmod(k, 2)
             z_i = pair + 7
             h_i = pair + 9
-            h_turn_now = second and h_i % 2 == 0 and 2 * NT <= h_i < B * NT
-            h_copy_now = (h_i - 1) % 2 == 0 and 2 * NT <= h_i - 1 < B * NT
+            h_turn_now = second and h_i % 2 == 0 and 3 * NT <= h_i < B * NT
+            h_copy_now = (h_i - 1) % 2 == 0 and 2 * NT < h_i - 1 < B * NT
+            if not second:
+                if pair in round_at:
+                    y_round(round_at[pair], nc.gpsimd)
+                if pair < 2:
+                    z_gain(NT + 2 * pair, nc.gpsimd, 0, P)
+                    z_gain(NT + 2 * pair + 1, nc.gpsimd, 0, P if pair == 0 else GP)
+                elif tile(z_i - 1):
+                    z_gain(z_i - 1, nc.gpsimd, 0, P if whole(pair) else GP)
             if second and unit(k + 2):
                 row_exp(k + 2)
             if unit(k - 2):
                 y_copy(k - 2)
-                if second:
-                    y_store(k - 3, 2)
             if not second and unit(k + 2):
                 row_exp(k + 2)
             if not second:
@@ -373,14 +425,6 @@ def tile_laatlabelwisetokenevidence_x2_kernel(
                     s_mm(k + 4)
                 if unit(k + 1):
                     p_mm(k + 1)
-            if not second:
-                if 0 <= k - 4 < LAST:
-                    y_round(k - 4, 2, nc.gpsimd)
-                if pair < 2:
-                    z_gain(NT + 2 * pair, nc.gpsimd, 0, P)
-                    z_gain(NT + 2 * pair + 1, nc.gpsimd, 0, P if pair == 0 else GP)
-                elif tile(z_i - 1):
-                    z_gain(z_i - 1, nc.gpsimd, 0, GP)
             if k == 0:
                 invert(0, 1)
                 product(0)
@@ -390,20 +434,22 @@ def tile_laatlabelwisetokenevidence_x2_kernel(
             if unit(k) and k > 0:
                 product(k)
             if second:
-                if unit(k - 5):
-                    finish_pair(k - 5)
+                if pair - LAG in round_at:
+                    y_quant(round_at[pair - LAG])
                 if pair < 2:
                     z_quant(NT + 2 * pair)
+                if h_copy_now:
+                    h_quant(h_i - 1, 2)
+                if tile(z_i) and not whole(pair + 1):
+                    z_gain(z_i, nc.vector, GP, P)
+                if pair < 2:
                     z_quant(NT + 2 * pair + 1)
                 elif tile(z_i - 1):
                     z_quant(z_i - 1)
-                if h_copy_now:
-                    h_quant(h_i - 1, 2)
-                if tile(z_i):
-                    z_gain(z_i, nc.vector, GP, P)
-                if unit(k + 1):
-                    invert(k + 1, 2)
+                invert(k + 1, 2)
 
+        NG = len(groups)
+        y_round(NG - 5, nc.gpsimd)
         y_copy(LAST - 2)
         row_exp(LAST + 2)
         p_mm(LAST + 1)
@@ -411,37 +457,33 @@ def tile_laatlabelwisetokenevidence_x2_kernel(
         turn(LAST - 1)
         lay_c(LAST, "z")
         p_mm(LAST + 2, "s")
-        y_round(LAST - 4, 2, nc.gpsimd)
         row_max(LAST + 3)
         product(LAST)
         turn(LAST)
         row_exp(LAST + 3)
         y_copy(LAST - 1)
-        y_store(LAST - 2, 2)
         lay_c(LAST + 1, "p")
         product(LAST + 1)
         turn(LAST + 1)
         p_mm(LAST + 3, "s")
         lay_c(LAST + 2, "t")
         invert(LAST + 2, 2)
-        finish_pair(LAST - 4)
+        if LAG:
+            y_quant(NG - 6)
+        y_quant(NG - 5)
         y_copy(LAST)
         y_copy(LAST + 1)
-        y_store(LAST, 2)
-        y_round(LAST - 2, 2, nc.gpsimd)
+        y_round(NG - 4, nc.gpsimd)
         for u in (LAST + 2, LAST + 3):
             product(u)
             if u == NU - 1:
                 lay_c(u, "s")
             turn(u)
             y_copy(u)
-            y_store(u, 1)
-        y_round(LAST, 2, nc.vector)
-        finish_pair(LAST - 2)
-        y_round(LAST + 2, 1, nc.vector)
-        y_quant(LAST, 2)
-        y_round(LAST + 3, 1, nc.vector)
-        y_quant(LAST + 2, 1)
-        y_quant(LAST + 3, 1)
-        codes_store(LAST, 4)
-        scales_store(B - 1, [nc.scalar, nc.sync, nc.scalar, nc.sync])
+        y_round(NG - 3, nc.vector)
+        y_quant(NG - 4)
+        y_round(NG - 2, nc.vector)
+        y_quant(NG - 3)
+        y_round(NG - 1, nc.vector)
+        y_quant(NG - 2)
+        y_quant(NG - 1)

@@ -22,6 +22,8 @@ BANKS = {"s": 3, "p": 2, "t": 2, "z": 1}
 YB = 1
 LAG = 0
 WH = ()
+SINGLES = 24
+CS = 20
 FLOPS = 2 * B * T * (D * A + A * L + D * L)
 
 
@@ -39,14 +41,14 @@ def tile_laatlabelwisetokenevidence_x2_kernel(
         ctx.enter_context(tc.manual_schedule())
 
         h_sb = {}
-        for b in range(B):
-            for hf in range(2):
-                h_sb[2 * b + hf] = const.tile([P, 2, D], BF16, name="h_sb_%d_%d" % (b, hf), align_bytes=64)
 
-        def load_h(hh):
-            b, hf = divmod(hh, 2)
+        def load_h(i, n):
+            b, t_i = divmod(i, NT)
+            rows = const.tile([P, n, D], BF16, name="h_sb_%d" % i, align_bytes=64)
             src = h[b].rearrange("(p t) d -> p t d", t=NT)
-            nc.sync.dma_start(out=h_sb[hh][:], in_=src[:, 2 * hf : 2 * hf + 2, :])
+            nc.sync.dma_start(out=rows[:], in_=src[:, t_i : t_i + n, :])
+            for d in range(n):
+                h_sb[i + d] = rows[:].bitcast(F32)[:, d, :]
 
         w_raw = const.tile([P, A], I32, name="w_raw", align_bytes=64)
         ws_raw = const.tile([P, A], U8, name="ws_raw", align_bytes=64)
@@ -75,15 +77,13 @@ def tile_laatlabelwisetokenevidence_x2_kernel(
             for r in range(4):
                 eng.dma_start(out=dst[r:P:32, :].bitcast(I32), in_=src[0, r:16:4, :].bitcast(I32))
 
-        load_h(0)
+        load_h(0, 2)
+        load_h(2, 2)
         nc.sync.dma_start(out=w_raw[:], in_=w_words[0].rearrange("p n t -> p (n t)").bitcast(I32))
-        load_h(1)
         load_scales(nc.sync, ws_raw, w_scales)
         nc.sync.dma_start(out=g_bf[:], in_=g.rearrange("(p t) -> p t", t=4))
-        load_h(2)
-        load_h(3)
-        load_h(4)
-        load_h(5)
+        for i in range(NT, 3 * NT, 2):
+            load_h(i, 2)
         nc.sync.dma_start(out=u_sb[:], in_=u_words[0].rearrange("p n t -> p (n t)").bitcast(I32))
         load_scales(nc.sync, us_sb, u_scales)
         nc.sync.dma_start(out=b_sb[:], in_=beta_words[0].rearrange("p n t -> p (n t)").bitcast(I32))
@@ -109,11 +109,10 @@ def tile_laatlabelwisetokenevidence_x2_kernel(
         h_bank, h_il, z_bank, z_t, z_b = {}, {}, {}, {}, {}
 
         def h_turn(i, n, tag):
-            words = h_sb[i // 2][:].bitcast(F32)
             h_bank[i] = psum.tile([P, n, 2, P], F32, name="h_bank", tag=tag, bufs=BANKS[tag])
             for d in range(n):
                 for e in range(2):
-                    nc.tensor.transpose(h_bank[i][:, d, e, :], words[:, i % 2 + d, e : D // 2 : 2], ident[:])
+                    nc.tensor.transpose(h_bank[i][:, d, e, :], h_sb[i + d][:, e : D // 2 : 2], ident[:])
 
         def h_copy(i, n):
             h_il[i] = stage.tile([P, n, P, 4], BF16, name="h_il", tag="h_il", bufs=6, align_bytes=64)
@@ -186,7 +185,7 @@ def tile_laatlabelwisetokenevidence_x2_kernel(
             round_at[pair] = len(groups)
             groups.append((done, n))
             done = done + n
-        groups.extend([(done, 2), (done + 2, 2), (done + 4, 1), (done + 5, 1)])
+        groups.extend([(u, 1) for u in range(done, NU)])
         assert done + 6 == NU
         group_of, y32 = {}, {}
         for gi in range(len(groups)):
@@ -280,25 +279,38 @@ def tile_laatlabelwisetokenevidence_x2_kernel(
             u0, n = groups[gi]
             k = u - u0
             nc.scalar.activation(out=y32[gi][:, :, P * k : P * (k + 1)], in_=t_ps[u][:], func=ACT.Copy, scale=float(T))
-            if k == n - 1:
-                cuts = sorted(set([u0, u0 + n, max(u0, NL * (u // NL))]))
-                for lo, hi in zip(cuts[:-1], cuts[1:]):
-                    b, j = divmod(lo, NL)
-                    dst = out_0[b].rearrange("(p t) l -> p t l", t=4)
-                    nc.sync.dma_start(
-                        out=dst[:, :, P * j : P * (j + hi - lo)], in_=y32[gi][:, :, P * (lo - u0) : P * (hi - u0)]
-                    )
+            if u < SINGLES and k == 1:
+                y_store(u - 1, 2)
+            elif SINGLES <= u < NU - 1:
+                y_store(u, 1)
+
+        def y_store(u, n):
+            gi = group_of[u]
+            k = u - groups[gi][0]
+            b, j = divmod(u, NL)
+            dst = out_0[b].rearrange("(p t) l -> p t l", t=4)
+            nc.sync.dma_start(out=dst[:, :, P * j : P * (j + n)], in_=y32[gi][:, :, P * k : P * (k + n)])
 
         def y_round(gi, eng):
             n = groups[gi][1]
             src = y32[gi][:].rearrange("p t (c i) -> p c t i", i=4)
             if eng is nc.gpsimd:
-                y16[gi] = stage.tile([P, n * P, 4], BF16, name="y16", tag="y16", bufs=YB, align_bytes=64)
+                tag, bufs = ("y16", 1) if n == 2 else ("y16_last", 6)
+                y16[gi] = stage.tile([P, n * P, 4], BF16, name=tag, tag=tag, bufs=bufs, align_bytes=64)
                 src = y32[gi][:].rearrange("p t l -> p l t")
                 eng.tensor_scalar(out=y16[gi][:], in0=src, scalar1=1.0, scalar2=1.0, op0=ALU.mult, op1=ALU.mult)
             else:
-                y16[gi] = stage.tile([P, n * P, 4], BF16, name="y16_last", tag="y16_last", bufs=3, align_bytes=64)
+                y16[gi] = stage.tile([P, n * P, 4], BF16, name="y16_last", tag="y16_last", bufs=6, align_bytes=64)
                 eng.tensor_copy(out=y16[gi][:].rearrange("p (c i) t -> p c t i", i=4), in_=src)
+
+        def y_round_bank(u, eng):
+            gi = group_of[u]
+            y16[gi] = stage.tile([P, P, 4], BF16, name="y16_last", tag="y16_last", bufs=6, align_bytes=64)
+            src = t_ps[u][:].rearrange("p t l -> p l t")
+            if eng is nc.vector:
+                eng.tensor_scalar(out=y16[gi][:], in0=src, scalar1=float(T), scalar2=None, op0=ALU.mult)
+            else:
+                eng.activation(out=y16[gi][:], in_=src, func=ACT.Copy, scale=float(T))
 
         def y_quant(gi):
             u0, n = groups[gi]
@@ -308,34 +320,35 @@ def tile_laatlabelwisetokenevidence_x2_kernel(
                 scales=o_scales[:, cols],
                 in_=y16[gi][:].rearrange("p l t -> p (l t)"),
             )
-            for q in range(u0 // 4, (u0 + n) // 4):
-                cols = slice(4 * P * q, 4 * P * (q + 1))
-                nc.sync.dma_start(out=out_words[:].bitcast(I32)[:, cols], in_=o_codes[:, cols])
-            for b in range(u0 // NL, (u0 + n) // NL):
-                for r in range(4):
-                    eng = nc.scalar if b == B - 1 and r % 2 == 0 else nc.sync
-                    eng.dma_start(
-                        out=out_2[0, 4 * r : 4 * r + 4, L * b : L * (b + 1)].bitcast(I32),
-                        in_=o_scales[32 * r : 32 * r + 4, L * b : L * (b + 1)].bitcast(I32),
-                    )
+
+        def codes_store(u0, n):
+            cols = slice(P * u0, P * (u0 + n))
+            nc.sync.dma_start(out=out_words[:].bitcast(I32)[:, cols], in_=o_codes[:, cols])
+
+        def scales_store(b, engines):
+            for r in range(4):
+                engines[r].dma_start(
+                    out=out_2[0, 4 * r : 4 * r + 4, L * b : L * (b + 1)].bitcast(I32),
+                    in_=o_scales[32 * r : 32 * r + 4, L * b : L * (b + 1)].bitcast(I32),
+                )
 
         GP = 64
         early = psum.tile([P, P], F32, name="early", tag="z", bufs=BANKS["z"])
         warm_up(early, 4)
         h_turn(0, 1, "t")
         h_turn(1, 1, "t")
-        warm_up(early, 1)
         prep_w()
         h_turn(2, 1, "p")
         h_turn(3, 1, "p")
+        warm_up(early, 1)
         for i in range(NT):
             h_copy(i, 1)
             h_quant(i, 1)
             z_mm(i, "s" if i < 3 else "z")
         nc.sync.dma_start(out=c_row[0:1, :], in_=c.rearrange("(o l) -> o l", o=1))
         nc.sync.dma_start(out=c_col_bf[:], in_=c[0:P].rearrange("(p o) -> p o", o=1))
-        for hh in range(6, 2 * B):
-            load_h(hh)
+        for i in range(3 * NT, B * NT, 2):
+            load_h(i, 2)
         for i in range(NT):
             z_tanh(i)
         later = psum.tile([P, P], F32, name="later", tag="s", bufs=BANKS["s"])
@@ -345,8 +358,10 @@ def tile_laatlabelwisetokenevidence_x2_kernel(
         h_copy(4, 2)
         h_copy(6, 2)
         h_turn(8, 2, "p")
+        h_turn(10, 2, "p")
         warm_up(later, 1)
         h_copy(8, 2)
+        h_copy(10, 2)
         for i in range(NT):
             z_gain(i, nc.vector, 0, P)
             if i == NT - 1:
@@ -368,12 +383,10 @@ def tile_laatlabelwisetokenevidence_x2_kernel(
             row_max(u)
         p_mm(0)
         z_mm(6, "z")
-        h_turn(10, 2, "t")
         row_exp(0)
         s_mm(3)
         row_exp(1)
         z_tanh(6)
-        h_copy(10, 2)
 
         def unit(u):
             return 0 <= u < NU
@@ -382,6 +395,14 @@ def tile_laatlabelwisetokenevidence_x2_kernel(
             return NT + 2 <= i < B * NT
 
         LAST = NU - 4
+        AHEAD = 19
+
+        def p_unit(k):
+            return k + 1 if k + 1 < AHEAD else k + 2
+
+        def p_bank(u):
+            return "z" if u >= AHEAD and (u - AHEAD) % 3 == 0 else "p"
+
         for k in range(LAST):
             pair, second = divmod(k, 2)
             z_i = pair + 7
@@ -403,10 +424,8 @@ def tile_laatlabelwisetokenevidence_x2_kernel(
             if not second and unit(k + 2):
                 row_exp(k + 2)
             if not second:
-                if unit(k + 1):
-                    p_mm(k + 1)
-                if unit(k + 4):
-                    s_mm(k + 4)
+                p_mm(p_unit(k), p_bank(p_unit(k)))
+                s_mm(k + 4)
                 if tile(z_i):
                     z_mm(z_i, "z")
                     z_tanh(z_i)
@@ -421,10 +440,14 @@ def tile_laatlabelwisetokenevidence_x2_kernel(
                 if h_turn_now:
                     h_turn(h_i, 2, "z")
                     h_copy(h_i, 2)
-                if unit(k + 4):
+                if h_turn_now or k + 1 > AHEAD:
                     s_mm(k + 4)
-                if unit(k + 1):
+                    p_mm(p_unit(k), p_bank(p_unit(k)))
+                else:
                     p_mm(k + 1)
+                    s_mm(k + 4)
+                    if k + 2 == AHEAD:
+                        p_mm(AHEAD, "z")
             if k == 0:
                 invert(0, 1)
                 product(0)
@@ -436,6 +459,12 @@ def tile_laatlabelwisetokenevidence_x2_kernel(
             if second:
                 if pair - LAG in round_at:
                     y_quant(round_at[pair - LAG])
+                    if k - 5 >= CS:
+                        codes_store(k - 5, 2)
+                    elif pair % 2 == 1:
+                        codes_store(k - 7, 4)
+                    if pair % 4 == 1:
+                        scales_store(pair // 4 - 1, [nc.sync] * 4)
                 if pair < 2:
                     z_quant(NT + 2 * pair)
                 if h_copy_now:
@@ -448,42 +477,46 @@ def tile_laatlabelwisetokenevidence_x2_kernel(
                     z_quant(z_i - 1)
                 invert(k + 1, 2)
 
-        NG = len(groups)
-        y_round(NG - 5, nc.gpsimd)
+        y_round(group_of[LAST - 4], nc.gpsimd)
         y_copy(LAST - 2)
+        y_round(group_of[LAST - 2], nc.gpsimd)
         row_exp(LAST + 2)
-        p_mm(LAST + 1)
         lay_c(LAST - 1, "t")
         turn(LAST - 1)
-        lay_c(LAST, "z")
-        p_mm(LAST + 2, "s")
+        y_copy(LAST - 1)
+        y_round(group_of[LAST - 1], nc.gpsimd)
+        p_mm(LAST + 2)
+        p_mm(LAST + 3, "s")
+        lay_c(LAST, "t")
         row_max(LAST + 3)
+        row_exp(LAST + 3)
         product(LAST)
         turn(LAST)
-        row_exp(LAST + 3)
-        y_copy(LAST - 1)
-        lay_c(LAST + 1, "p")
+        invert(LAST + 2, 1)
         product(LAST + 1)
+        lay_c(LAST + 1, "s")
         turn(LAST + 1)
-        p_mm(LAST + 3, "s")
-        lay_c(LAST + 2, "t")
-        invert(LAST + 2, 2)
-        if LAG:
-            y_quant(NG - 6)
-        y_quant(NG - 5)
-        y_copy(LAST)
-        y_copy(LAST + 1)
-        y_round(NG - 4, nc.gpsimd)
-        for u in (LAST + 2, LAST + 3):
-            product(u)
-            if u == NU - 1:
-                lay_c(u, "s")
-            turn(u)
+        product(LAST + 2)
+        lay_c(LAST + 2, "z")
+        turn(LAST + 2)
+        invert(LAST + 3, 1)
+        product(LAST + 3)
+        lay_c(LAST + 3, "s")
+        turn(LAST + 3)
+        for u in range(LAST, NU):
             y_copy(u)
-        y_round(NG - 3, nc.vector)
-        y_quant(NG - 4)
-        y_round(NG - 2, nc.vector)
-        y_quant(NG - 3)
-        y_round(NG - 1, nc.vector)
-        y_quant(NG - 2)
-        y_quant(NG - 1)
+        y_round_bank(LAST, nc.vector)
+        y_round_bank(LAST + 2, nc.scalar)
+        for u in (LAST - 4, LAST - 2, LAST - 1):
+            y_quant(group_of[u])
+        codes_store(LAST - 4, 4)
+        y_store(NU - 1, 1)
+        y_round(group_of[LAST + 1], nc.vector)
+        y_quant(group_of[LAST])
+        y_round(group_of[LAST + 3], nc.vector)
+        y_quant(group_of[LAST + 1])
+        codes_store(LAST, 2)
+        y_quant(group_of[LAST + 3])
+        y_quant(group_of[LAST + 2])
+        codes_store(LAST + 2, 2)
+        scales_store(B - 1, [nc.scalar, nc.sync, nc.scalar, nc.sync])

@@ -61,17 +61,11 @@ def tile_laatlabelwisetokenevidence_x2_kernel(
         spread = const.tile([P, P], BF16, name="spread", align_bytes=64)
         c_col_bf = const.tile([P, 1], BF16, name="c_col_bf")
         c_col = const.tile([P, 1], F32, name="c_col")
-        zeros = const.tile([P, P], F32, name="zeros", align_bytes=64)
-        nc.vector.memset(zeros[:], 0.0)
         nc.vector.memset(ws_raw[:].bitcast(I32), 0)
         nc.vector.memset(c_row[:], 0.0)
         nc.vector.memset(us_sb[:].bitcast(I32), 0)
         nc.vector.memset(bs_sb[:].bitcast(I32), 0)
         nc.vector.memset(spread[:], 1.0 / T)
-
-        def warm_up(bank, n):
-            for i in range(n):
-                nc.tensor.matmul(out=bank[:], lhsT=zeros[:], rhs=zeros[:], start=True, stop=True)
 
         def load_scales(eng, dst, src):
             for r in range(4):
@@ -333,14 +327,11 @@ def tile_laatlabelwisetokenevidence_x2_kernel(
                 )
 
         GP = 64
-        early = psum.tile([P, P], F32, name="early", tag="z", bufs=BANKS["z"])
-        warm_up(early, 4)
         h_turn(0, 1, "t")
         h_turn(1, 1, "t")
         prep_w()
         h_turn(2, 1, "p")
         h_turn(3, 1, "p")
-        warm_up(early, 1)
         for i in range(NT):
             h_copy(i, 1)
             h_quant(i, 1)
@@ -351,15 +342,12 @@ def tile_laatlabelwisetokenevidence_x2_kernel(
             load_h(i, 2)
         for i in range(NT):
             z_tanh(i)
-        later = psum.tile([P, P], F32, name="later", tag="s", bufs=BANKS["s"])
         h_turn(4, 2, "t")
         h_turn(6, 2, "t")
-        warm_up(later, 2)
         h_copy(4, 2)
         h_copy(6, 2)
         h_turn(8, 2, "p")
         h_turn(10, 2, "p")
-        warm_up(later, 1)
         h_copy(8, 2)
         h_copy(10, 2)
         for i in range(NT):

@@ -59,9 +59,9 @@ def tile_laatlabelwisetokenevidence_x2_kernel(
         g_bf = const.tile([P, 4], BF16, name="g_bf")
         c_row = const.tile([P, L], BF16, name="c_row", align_bytes=64)
         spread = const.tile([P, P], BF16, name="spread", align_bytes=64)
-        c_col_bf = const.tile([P, 1], BF16, name="c_col_bf")
-        c_col = const.tile([P, 1], F32, name="c_col")
+        ident = const.tile([P, P], F32, name="ident", align_bytes=64)
         nc.vector.memset(ws_raw[:].bitcast(I32), 0)
+        nc.vector.memset(ident[:], 0.0)
         nc.vector.memset(c_row[:], 0.0)
         nc.vector.memset(us_sb[:].bitcast(I32), 0)
         nc.vector.memset(bs_sb[:].bitcast(I32), 0)
@@ -72,8 +72,8 @@ def tile_laatlabelwisetokenevidence_x2_kernel(
                 eng.dma_start(out=dst[r:P:32, :].bitcast(I32), in_=src[0, r:16:4, :].bitcast(I32))
 
         load_h(0, 2)
-        load_h(2, 2)
         nc.sync.dma_start(out=w_raw[:], in_=w_words[0].rearrange("p n t -> p (n t)").bitcast(I32))
+        load_h(2, 2)
         load_scales(nc.sync, ws_raw, w_scales)
         nc.sync.dma_start(out=g_bf[:], in_=g.rearrange("(p t) -> p t", t=4))
         for i in range(NT, 3 * NT, 2):
@@ -83,8 +83,7 @@ def tile_laatlabelwisetokenevidence_x2_kernel(
         nc.sync.dma_start(out=b_sb[:], in_=beta_words[0].rearrange("p n t -> p (n t)").bitcast(I32))
         load_scales(nc.sync, bs_sb, beta_scales)
 
-        ident = const.tile([P, P], F32, name="ident", align_bytes=64)
-        make_identity(nc, ident[:])
+        make_identity(nc, ident[:], nomemset=True)
         w_sb = const.tile([P, 4, P], I32, name="w_sb", align_bytes=64)
         ws_sb = const.tile([P, 4, P], U8, name="ws_sb", align_bytes=64)
         g_sb = const.tile([P, 4], F32, name="g_sb")
@@ -92,7 +91,6 @@ def tile_laatlabelwisetokenevidence_x2_kernel(
         def prep_w():
             nc.vector.tensor_copy(out=ws_sb[:], in_=ws_raw[:].rearrange("p (m t) -> p t m", t=4))
             nc.vector.tensor_copy(out=w_sb[:], in_=w_raw[:].rearrange("p (m t) -> p t m", t=4))
-            nc.vector.tensor_copy(out=g_sb[:], in_=g_bf[:])
 
         h_codes, h_scales, z_codes, z_scales = {}, {}, {}, {}
         for b in range(B):
@@ -142,7 +140,7 @@ def tile_laatlabelwisetokenevidence_x2_kernel(
 
         def z_gain(i, eng, lo, hi):
             if i not in z_b:
-                tag, bufs = ("y16", YB) if i in (NT, NT + 2) else ("z_b", NT)
+                tag, bufs = ("y16", YB) if i in (NT, NT + 3) else ("z_b", NT)
                 z_b[i] = stage.tile([P, P, 4], BF16, name=tag, tag=tag, bufs=bufs, align_bytes=64)
             eng.tensor_tensor(
                 out=z_b[i][:, lo:hi, :],
@@ -238,17 +236,6 @@ def tile_laatlabelwisetokenevidence_x2_kernel(
         def lay_c(u, tag):
             j = u % NL
             t_ps[u] = psum.tile([P, 4, P], F32, name="t_ps", tag=tag, bufs=BANKS[tag])
-            if j == 0 and u > 0:
-                for t in range(4):
-                    nc.tensor.matmul(
-                        out=t_ps[u][:, t, :],
-                        lhsT=c_col[:].to_broadcast([P, P]),
-                        rhs=ident[:],
-                        is_transpose=True,
-                        start=(t == 0),
-                        stop=False,
-                    )
-                return
             nc.tensor.matmul(
                 out=t_ps[u][:],
                 lhsT=spread[:],
@@ -336,8 +323,8 @@ def tile_laatlabelwisetokenevidence_x2_kernel(
             h_copy(i, 1)
             h_quant(i, 1)
             z_mm(i, "s" if i < 3 else "z")
+        nc.vector.tensor_copy(out=g_sb[:], in_=g_bf[:])
         nc.sync.dma_start(out=c_row[0:1, :], in_=c.rearrange("(o l) -> o l", o=1))
-        nc.sync.dma_start(out=c_col_bf[:], in_=c[0:P].rearrange("(p o) -> p o", o=1))
         for i in range(3 * NT, B * NT, 2):
             load_h(i, 2)
         for i in range(NT):
@@ -351,20 +338,18 @@ def tile_laatlabelwisetokenevidence_x2_kernel(
         h_copy(8, 2)
         h_copy(10, 2)
         for i in range(NT):
-            z_gain(i, nc.vector, 0, P)
             if i == NT - 1:
                 h_quant(4, 2)
+            z_gain(i, nc.vector, 0, P)
             if i > 0:
                 z_quant(i - 1)
         z_quant(NT - 1)
-        h_quant(6, 2)
-        h_quant(8, 2)
-        nc.gpsimd.tensor_scalar(out=c_col[:], in0=c_col_bf[:], scalar1=1.0 / T, scalar2=1.0, op0=ALU.mult, op1=ALU.mult)
-        z_mm(4, "t")
-        z_tanh(4)
+        for i in range(6, 3 * NT, 2):
+            h_quant(i, 2)
+        for i in (4, 5):
+            z_mm(i, "t")
+            z_tanh(i)
         s_mm(0)
-        z_mm(5, "t")
-        z_tanh(5)
         s_mm(1)
         s_mm(2)
         for u in range(3):
@@ -396,15 +381,17 @@ def tile_laatlabelwisetokenevidence_x2_kernel(
             z_i = pair + 7
             h_i = pair + 9
             h_turn_now = second and h_i % 2 == 0 and 3 * NT <= h_i < B * NT
-            h_copy_now = (h_i - 1) % 2 == 0 and 2 * NT < h_i - 1 < B * NT
+            h_copy_now = (h_i - 1) % 2 == 0 and 3 * NT <= h_i - 1 < B * NT
             if not second:
                 if pair in round_at:
                     y_round(round_at[pair], nc.gpsimd)
-                if pair < 2:
-                    z_gain(NT + 2 * pair, nc.gpsimd, 0, P)
-                    z_gain(NT + 2 * pair + 1, nc.gpsimd, 0, P if pair == 0 else GP)
+                if pair == 0:
+                    for i in (4, 5, 6):
+                        z_gain(i, nc.gpsimd, 0, P)
+                elif pair == 1:
+                    z_gain(7, nc.gpsimd, 0, P)
                 elif tile(z_i - 1):
-                    z_gain(z_i - 1, nc.gpsimd, 0, P if whole(pair) else GP)
+                    z_gain(z_i - 1, nc.gpsimd, 0, GP)
             if second and unit(k + 2):
                 row_exp(k + 2)
             if unit(k - 2):
@@ -453,15 +440,16 @@ def tile_laatlabelwisetokenevidence_x2_kernel(
                         codes_store(k - 7, 4)
                     if pair % 4 == 1:
                         scales_store(pair // 4 - 1, [nc.sync] * 4)
-                if pair < 2:
-                    z_quant(NT + 2 * pair)
+                if pair == 0:
+                    for i in (4, 5, 6):
+                        z_quant(i)
+                elif pair == 1:
+                    z_quant(7)
                 if h_copy_now:
                     h_quant(h_i - 1, 2)
-                if tile(z_i) and not whole(pair + 1):
+                if tile(z_i) and pair > 0:
                     z_gain(z_i, nc.vector, GP, P)
-                if pair < 2:
-                    z_quant(NT + 2 * pair + 1)
-                elif tile(z_i - 1):
+                if pair > 1 and tile(z_i - 1):
                     z_quant(z_i - 1)
                 invert(k + 1, 2)
 

@@ -71,10 +71,11 @@ def tile_laatlabelwisetokenevidence_x2_kernel(
             for r in range(4):
                 eng.dma_start(out=dst[r:P:32, :].bitcast(I32), in_=src[0, r:16:4, :].bitcast(I32))
 
-        load_h(0, 2)
+        load_h(0, 1)
         nc.sync.dma_start(out=w_raw[:], in_=w_words[0].rearrange("p n t -> p (n t)").bitcast(I32))
-        load_h(2, 2)
         load_scales(nc.sync, ws_raw, w_scales)
+        load_h(1, 1)
+        load_h(2, 2)
         nc.sync.dma_start(out=g_bf[:], in_=g.rearrange("(p t) -> p t", t=4))
         for i in range(NT, 3 * NT, 2):
             load_h(i, 2)

@@ -279,8 +279,8 @@ def tile_laatlabelwisetokenevidence_x2_kernel(
             if eng is nc.gpsimd:
                 tag, bufs = ("y16", 1) if n == 2 else ("y16_last", 6)
                 y16[gi] = stage.tile([P, n * P, 4], BF16, name=tag, tag=tag, bufs=bufs, align_bytes=64)
-                src = y32[gi][:].rearrange("p t l -> p l t")
-                eng.tensor_scalar(out=y16[gi][:], in0=src, scalar1=1.0, scalar2=1.0, op0=ALU.mult, op1=ALU.mult)
+                dst = y16[gi][:].rearrange("p (c i) t -> p c t i", i=4)
+                eng.tensor_scalar(out=dst, in0=src, scalar1=1.0, scalar2=1.0, op0=ALU.mult, op1=ALU.mult)
             else:
                 y16[gi] = stage.tile([P, n * P, 4], BF16, name="y16_last", tag="y16_last", bufs=6, align_bytes=64)
                 eng.tensor_copy(out=y16[gi][:].rearrange("p (c i) t -> p c t i", i=4), in_=src)
@@ -314,7 +314,7 @@ def tile_laatlabelwisetokenevidence_x2_kernel(
                     in_=o_scales[32 * r : 32 * r + 4, L * b : L * (b + 1)].bitcast(I32),
                 )
 
-        GP = 64
+        GP = 80
         h_turn(0, 1, "t")
         h_turn(1, 1, "t")
         prep_w()

@@ -314,7 +314,7 @@ def tile_laatlabelwisetokenevidence_x2_kernel(
                     in_=o_scales[32 * r : 32 * r + 4, L * b : L * (b + 1)].bitcast(I32),
                 )
 
-        GP = 80
+        GP = 68
         h_turn(0, 1, "t")
         h_turn(1, 1, "t")
         prep_w()

@@ -20,10 +20,10 @@ AX = mybir.AxisListType
 
 BANKS = {"s": 3, "p": 2, "t": 2, "z": 1}
 YB = 1
-LAG = 0
-WH = ()
+HELD = (4, 7)
+VS = 40
+BY_VECTOR = (3,)
 SINGLES = 24
-CS = 20
 FLOPS = 2 * B * T * (D * A + A * L + D * L)
 
 
@@ -135,14 +135,22 @@ def tile_laatlabelwisetokenevidence_x2_kernel(
                     stop=True,
                 )
 
+        def z_span(i):
+            return (i, 1) if i < 2 * NT else (i - i % 2, 2)
+
         def z_tanh(i):
-            z_t[i] = stage.tile([P, P, 4], F32, name="z_t", tag="z_t")
-            nc.scalar.activation(out=z_t[i][:], in_=z_bank[i][:].rearrange("m t n -> m n t"), func=ACT.Tanh)
+            i0, n = z_span(i)
+            if i == i0:
+                z_t[i0] = stage.tile([P, n * P, 4], F32, name="z_t", tag="z_t")
+            d = i - i0
+            nc.scalar.activation(
+                out=z_t[i0][:, P * d : P * (d + 1), :], in_=z_bank[i][:].rearrange("m t n -> m n t"), func=ACT.Tanh
+            )
 
         def z_gain(i, eng, lo, hi):
             if i not in z_b:
-                tag, bufs = ("y16", YB) if i in (NT, NT + 3) else ("z_b", NT)
-                z_b[i] = stage.tile([P, P, 4], BF16, name=tag, tag=tag, bufs=bufs, align_bytes=64)
+                tag, bufs = ("y16", YB) if i in HELD else ("z_b", NT)
+                z_b[i] = stage.tile([P, z_span(i)[1] * P, 4], BF16, name=tag, tag=tag, bufs=bufs, align_bytes=64)
             eng.tensor_tensor(
                 out=z_b[i][:, lo:hi, :],
                 in0=z_t[i][:, lo:hi, :],
@@ -152,7 +160,7 @@ def tile_laatlabelwisetokenevidence_x2_kernel(
 
         def z_quant(i):
             b, t_i = divmod(i, NT)
-            cols = slice(P * t_i, P * (t_i + 1))
+            cols = slice(P * t_i, P * (t_i + z_span(i)[1]))
             nc.vector.quantize_mx(
                 out=z_codes[b][:, cols].bitcast(FP8X4),
                 scales=z_scales[b][:, cols],
@@ -165,16 +173,12 @@ def tile_laatlabelwisetokenevidence_x2_kernel(
         o_codes = const.tile([P, NU * P], I32, name="o_codes", align_bytes=64)
         o_scales = const.tile([P, NU * P], U8, name="o_scales", align_bytes=64)
 
-        def whole(pair):
-            return pair in WH
-
         groups, round_at = [], {}
         done = 0
         for pair in range(2, NU // 2 - 1):
-            if pair + 6 < B * NT:
-                n = 1 if whole(pair) else 2
-            else:
-                n = min(3, 2 * pair - 2 - done)
+            if pair % 2 == 1 and pair + 6 < B * NT:
+                continue
+            n = min(4 if pair + 6 < B * NT else 3, 2 * pair - 2 - done)
             round_at[pair] = len(groups)
             groups.append((done, n))
             done = done + n
@@ -187,10 +191,10 @@ def tile_laatlabelwisetokenevidence_x2_kernel(
             for u in range(u0, u0 + n):
                 group_of[u] = gi
 
-        def s_mm(u):
+        def s_mm(u, tag="s"):
             b, j = divmod(u, NL)
             cols = slice(P * j, P * (j + 1))
-            s_ps[u] = psum.tile([P, T], F32, name="s_ps", tag="s", bufs=BANKS["s"])
+            s_ps[u] = psum.tile([P, T], F32, name="s_ps", tag=tag, bufs=BANKS[tag])
             nc.tensor.matmul_mx(
                 out=s_ps[u][:],
                 lhsT=u_sb[:, cols].bitcast(FP8X4),
@@ -237,6 +241,8 @@ def tile_laatlabelwisetokenevidence_x2_kernel(
         def lay_c(u, tag):
             j = u % NL
             t_ps[u] = psum.tile([P, 4, P], F32, name="t_ps", tag=tag, bufs=BANKS[tag])
+            if u in BY_VECTOR:
+                return
             nc.tensor.matmul(
                 out=t_ps[u][:],
                 lhsT=spread[:],
@@ -252,16 +258,30 @@ def tile_laatlabelwisetokenevidence_x2_kernel(
                     lhsT=vt[u][:, P * t : P * (t + 1)],
                     rhs=ident[:],
                     is_transpose=True,
-                    start=False,
-                    stop=(t == 3),
+                    start=(u in BY_VECTOR),
+                    stop=(t == 3 or u in BY_VECTOR),
                 )
 
         def y_copy(u):
             gi = group_of[u]
             u0, n = groups[gi]
             k = u - u0
-            nc.scalar.activation(out=y32[gi][:, :, P * k : P * (k + 1)], in_=t_ps[u][:], func=ACT.Copy, scale=float(T))
-            if u < SINGLES and k == 1:
+            if u in BY_VECTOR:
+                nc.vector.scalar_tensor_tensor(
+                    out=y32[gi][:, :, P * k : P * (k + 1)],
+                    in0=t_ps[u][:],
+                    scalar=float(T),
+                    in1=c_all[u % NL][:].unsqueeze(1).to_broadcast([P, 4, P]),
+                    op0=ALU.mult,
+                    op1=ALU.add,
+                )
+            else:
+                nc.scalar.activation(
+                    out=y32[gi][:, :, P * k : P * (k + 1)], in_=t_ps[u][:], func=ACT.Copy, scale=float(T)
+                )
+            if u < SINGLES and n == 3 and k == 2:
+                y_store(u, 1)
+            elif u < SINGLES and k % 2 == 1:
                 y_store(u - 1, 2)
             elif SINGLES <= u < NU - 1:
                 y_store(u, 1)
@@ -277,7 +297,7 @@ def tile_laatlabelwisetokenevidence_x2_kernel(
             n = groups[gi][1]
             src = y32[gi][:].rearrange("p t (c i) -> p c t i", i=4)
             if eng is nc.gpsimd:
-                tag, bufs = ("y16", 1) if n == 2 else ("y16_last", 6)
+                tag, bufs = ("y16", 1) if n >= 2 else ("y16_last", 6)
                 y16[gi] = stage.tile([P, n * P, 4], BF16, name=tag, tag=tag, bufs=bufs, align_bytes=64)
                 dst = y16[gi][:].rearrange("p (c i) t -> p c t i", i=4)
                 eng.tensor_scalar(out=dst, in0=src, scalar1=1.0, scalar2=1.0, op0=ALU.mult, op1=ALU.mult)
@@ -314,7 +334,6 @@ def tile_laatlabelwisetokenevidence_x2_kernel(
                     in_=o_scales[32 * r : 32 * r + 4, L * b : L * (b + 1)].bitcast(I32),
                 )
 
-        GP = 68
         h_turn(0, 1, "t")
         h_turn(1, 1, "t")
         prep_w()
@@ -328,6 +347,10 @@ def tile_laatlabelwisetokenevidence_x2_kernel(
         nc.sync.dma_start(out=c_row[0:1, :], in_=c.rearrange("(o l) -> o l", o=1))
         for i in range(3 * NT, B * NT, 2):
             load_h(i, 2)
+        c_all = {}
+        for j in sorted(set(u % NL for u in BY_VECTOR)):
+            c_all[j] = const.tile([P, P], BF16, name="c_all_%d" % j, align_bytes=64)
+            nc.sync.dma_start(out=c_all[j][:], in_=c[P * j : P * (j + 1)].partition_broadcast(P))
         for i in range(NT):
             z_tanh(i)
         h_turn(4, 2, "t")
@@ -351,107 +374,191 @@ def tile_laatlabelwisetokenevidence_x2_kernel(
             z_mm(i, "t")
             z_tanh(i)
         s_mm(0)
+        z_mm(6, "z")
+        z_tanh(6)
         s_mm(1)
         s_mm(2)
         for u in range(3):
             row_max(u)
         p_mm(0)
-        z_mm(6, "z")
+        s_mm(3, "t")
         row_exp(0)
-        s_mm(3)
         row_exp(1)
-        z_tanh(6)
 
         def unit(u):
             return 0 <= u < NU
 
-        def tile(i):
-            return NT + 2 <= i < B * NT
-
         LAST = NU - 4
-        AHEAD = 19
-
-        def p_unit(k):
-            return k + 1 if k + 1 < AHEAD else k + 2
+        AHEAD = 22
 
         def p_bank(u):
-            return "z" if u >= AHEAD and (u - AHEAD) % 3 == 0 else "p"
+            return "z" if (u - AHEAD) % 3 == 0 else "p"
 
-        for k in range(LAST):
+        def y_out(gi):
+            y_quant(gi)
+            u0, n = groups[gi]
+            codes_store(u0, n)
+            if (u0 + n) // NL > u0 // NL:
+                scales_store(u0 // NL, [nc.sync] * 4)
+
+        def share(j):
+            return 0 if j == 1 or 4 * j - 1 in BY_VECTOR else VS
+
+        for k in range(4):
             pair, second = divmod(k, 2)
-            z_i = pair + 7
-            h_i = pair + 9
-            h_turn_now = second and h_i % 2 == 0 and 3 * NT <= h_i < B * NT
-            h_copy_now = (h_i - 1) % 2 == 0 and 3 * NT <= h_i - 1 < B * NT
-            if not second:
-                if pair in round_at:
-                    y_round(round_at[pair], nc.gpsimd)
-                if pair == 0:
-                    for i in (4, 5, 6):
-                        z_gain(i, nc.gpsimd, 0, P)
-                elif pair == 1:
-                    z_gain(7, nc.gpsimd, 0, P)
-                elif tile(z_i - 1):
-                    z_gain(z_i - 1, nc.gpsimd, 0, GP)
-            if second and unit(k + 2):
+            if k == 0:
+                for i in (4, 5, 6):
+                    z_gain(i, nc.gpsimd, 0, P)
+            if k == 2:
+                z_gain(7, nc.gpsimd, 0, P)
+            if second:
                 row_exp(k + 2)
+            if k == 1:
+                z_tanh(7)
             if unit(k - 2):
                 y_copy(k - 2)
-            if not second and unit(k + 2):
-                row_exp(k + 2)
             if not second:
-                p_mm(p_unit(k), p_bank(p_unit(k)))
-                s_mm(k + 4)
-                if tile(z_i):
-                    z_mm(z_i, "z")
-                    z_tanh(z_i)
+                row_exp(k + 2)
+                if k == 2:
+                    h_copy(12, 2)
+                p_mm(k + 1)
+                if pair == 0:
+                    s_mm(k + 4)
+                z_mm(pair + 7, "z")
+                if pair > 0:
+                    s_mm(k + 4)
+                if pair > 0:
+                    z_tanh(pair + 7)
                 for u in (k - 1, k):
                     if unit(u):
                         lay_c(u, "t")
                 if unit(k - 1):
                     turn(k - 1)
-            else:
-                if unit(k - 1):
-                    turn(k - 1)
-                if h_turn_now:
-                    h_turn(h_i, 2, "z")
-                    h_copy(h_i, 2)
-                if h_turn_now or k + 1 > AHEAD:
-                    s_mm(k + 4)
-                    p_mm(p_unit(k), p_bank(p_unit(k)))
                 else:
-                    p_mm(k + 1)
-                    s_mm(k + 4)
-                    if k + 2 == AHEAD:
-                        p_mm(AHEAD, "z")
+                    h_turn(12, 2, "s")
+            elif k == 1:
+                turn(k - 1)
+                p_mm(k + 1)
+                s_mm(k + 4)
+            else:
+                turn(k - 1)
+                s_mm(k + 4)
+                p_mm(k + 1)
+                z_mm(9, "z")
             if k == 0:
                 invert(0, 1)
+                row_max(3)
                 product(0)
                 invert(1, 1)
-            if unit(k + 3):
+            if k > 0:
                 row_max(k + 3)
-            if unit(k) and k > 0:
+            if k > 0:
                 product(k)
+            if k == 1:
+                for i in (4, 5, 6):
+                    z_quant(i)
+            if k == 3:
+                z_quant(7)
+                h_quant(12, 2)
             if second:
-                if pair - LAG in round_at:
-                    y_quant(round_at[pair - LAG])
-                    if k - 5 >= CS:
-                        codes_store(k - 5, 2)
-                    elif pair % 2 == 1:
-                        codes_store(k - 7, 4)
-                    if pair % 4 == 1:
-                        scales_store(pair // 4 - 1, [nc.sync] * 4)
-                if pair == 0:
-                    for i in (4, 5, 6):
-                        z_quant(i)
-                elif pair == 1:
-                    z_quant(7)
-                if h_copy_now:
-                    h_quant(h_i - 1, 2)
-                if tile(z_i) and pair > 0:
-                    z_gain(z_i, nc.vector, GP, P)
-                if pair > 1 and tile(z_i - 1):
-                    z_quant(z_i - 1)
+                invert(k + 1, 2)
+        row_exp(6)
+        z_tanh(9)
+        p_mm(5)
+        s_mm(8)
+        lay_c(3, "t")
+        turn(3)
+
+        for j in range(1, B + 1):
+            k = 4 * j
+            z_i = 2 * j + 6
+            h_i = 2 * j + 12
+            y_round(round_at[2 * j], nc.gpsimd)
+            row_max(k + 3)
+            if j > 1:
+                z_tanh(z_i + 1)
+            z_gain(z_i, nc.gpsimd, share(j), 2 * P)
+            row_exp(k + 3)
+            product(k)
+            if k - 2 not in BY_VECTOR:
+                y_copy(k - 2)
+            if h_i < B * NT:
+                h_turn(h_i, 2, "z")
+            s_mm(k + 5)
+            p_mm(k + 2)
+            row_max(k + 4)
+            product(k + 1)
+            if k - 1 not in BY_VECTOR:
+                y_copy(k - 1)
+            if h_i < B * NT:
+                h_copy(h_i, 2)
+            row_exp(k + 4)
+            for u in (k - 2, k - 1):
+                if u in BY_VECTOR:
+                    y_copy(u)
+            invert(k + 2, 2)
+            s_mm(k + 6)
+            p_mm(k + 3)
+            if j < B:
+                z_mm(z_i + 2, "z")
+            lay_c(k, "t")
+            lay_c(k + 1, "t")
+            turn(k)
+            turn(k + 1)
+            row_max(k + 5)
+            row_exp(k + 5)
+            if j < B:
+                z_tanh(z_i + 2)
+            product(k + 2)
+            row_max(k + 6)
+            product(k + 3)
+            y_copy(k)
+            y_copy(k + 1)
+            row_exp(k + 6)
+            z_quant(z_i)
+            y_out(round_at[2 * j])
+            if h_i < B * NT:
+                h_quant(h_i, 2)
+            if j < B and share(j + 1) > 0:
+                z_gain(z_i + 2, nc.vector, 0, VS)
+            invert(k + 4, 2)
+            s_mm(k + 7)
+            p_mm(k + 4)
+            if j < B:
+                z_mm(z_i + 3, "z")
+            p_mm(k + 5)
+            if j < B:
+                s_mm(k + 8)
+            last = k + 3 if j < B else k + 2
+            for u in range(k + 2, last + 1):
+                lay_c(u, "t")
+            for u in range(k + 2, last + 1):
+                turn(u)
+
+        FIRST = 4 * B + 4
+        for k in range(FIRST, LAST):
+            pair, second = divmod(k, 2)
+            if not second:
+                y_round(round_at[pair], nc.gpsimd)
+            else:
+                row_exp(k + 2)
+            y_copy(k - 2)
+            if not second:
+                if k > FIRST:
+                    row_exp(k + 2)
+                p_mm(k + 2, p_bank(k + 2))
+                s_mm(k + 4)
+                lay_c(k - 1, "t")
+                lay_c(k, "t")
+                turn(k - 1)
+            else:
+                turn(k - 1)
+                s_mm(k + 4)
+                p_mm(k + 2, p_bank(k + 2))
+            row_max(k + 3)
+            product(k)
+            if second:
+                y_out(round_at[pair])
                 invert(k + 1, 2)
 
         y_round(group_of[LAST - 4], nc.gpsimd)

@@ -506,8 +506,11 @@ def tile_laatlabelwisetokenevidence_x2_kernel(
             turn(k)
             turn(k + 1)
             row_max(k + 5)
+            if j == 1:
+                z_tanh(z_i + 2)
+                z_gain(z_i + 2, nc.gpsimd, 0, VS)
             row_exp(k + 5)
-            if j < B:
+            if 1 < j < B:
                 z_tanh(z_i + 2)
             product(k + 2)
             row_max(k + 6)
@@ -515,11 +518,11 @@ def tile_laatlabelwisetokenevidence_x2_kernel(
             y_copy(k)
             y_copy(k + 1)
             row_exp(k + 6)
-            z_quant(z_i)
             y_out(round_at[2 * j])
+            z_quant(z_i)
             if h_i < B * NT:
                 h_quant(h_i, 2)
-            if j < B and share(j + 1) > 0:
+            if 1 < j < B and share(j + 1) > 0:
                 z_gain(z_i + 2, nc.vector, 0, VS)
             invert(k + 4, 2)
             s_mm(k + 7)
@@ -587,19 +590,22 @@ def tile_laatlabelwisetokenevidence_x2_kernel(
         product(LAST + 3)
         lay_c(LAST + 3, "s")
         turn(LAST + 3)
-        for u in range(LAST, NU):
-            y_copy(u)
-        y_round_bank(LAST, nc.vector)
+        y_copy(LAST + 0)
+        y_round(group_of[LAST + 0], nc.gpsimd)
+        y_copy(LAST + 1)
+        y_copy(LAST + 2)
+        y_copy(LAST + 3)
         y_round_bank(LAST + 2, nc.scalar)
-        for u in (LAST - 4, LAST - 2, LAST - 1):
-            y_quant(group_of[u])
+        y_round_bank(LAST + 1, nc.vector)
+        y_quant(group_of[LAST - 4])
+        y_quant(group_of[LAST - 2])
+        y_quant(group_of[LAST - 1])
         codes_store(LAST - 4, 4)
-        y_store(NU - 1, 1)
-        y_round(group_of[LAST + 1], nc.vector)
-        y_quant(group_of[LAST])
+        y_store(LAST + 3, 1)
+        y_quant(group_of[LAST + 0])
         y_round(group_of[LAST + 3], nc.vector)
         y_quant(group_of[LAST + 1])
-        codes_store(LAST, 2)
+        codes_store(LAST + 0, 2)
         y_quant(group_of[LAST + 3])
         y_quant(group_of[LAST + 2])
         codes_store(LAST + 2, 2)

@@ -262,7 +262,7 @@ def tile_laatlabelwisetokenevidence_x2_kernel(
                     stop=(t == 3 or u in BY_VECTOR),
                 )
 
-        def y_copy(u):
+        def y_copy(u, eng=nc.scalar):
             gi = group_of[u]
             u0, n = groups[gi]
             k = u - u0
@@ -274,6 +274,10 @@ def tile_laatlabelwisetokenevidence_x2_kernel(
                     in1=c_all[u % NL][:].unsqueeze(1).to_broadcast([P, 4, P]),
                     op0=ALU.mult,
                     op1=ALU.add,
+                )
+            elif eng is nc.vector:
+                nc.vector.tensor_scalar(
+                    out=y32[gi][:, :, P * k : P * (k + 1)], in0=t_ps[u][:], scalar1=float(T), scalar2=None, op0=ALU.mult
                 )
             else:
                 nc.scalar.activation(
@@ -568,40 +572,40 @@ def tile_laatlabelwisetokenevidence_x2_kernel(
         y_copy(LAST - 2)
         y_round(group_of[LAST - 2], nc.gpsimd)
         row_exp(LAST + 2)
-        lay_c(LAST - 1, "t")
-        turn(LAST - 1)
-        y_copy(LAST - 1)
-        y_round(group_of[LAST - 1], nc.gpsimd)
         p_mm(LAST + 2)
-        p_mm(LAST + 3, "s")
+        lay_c(LAST - 1, "t")
         lay_c(LAST, "t")
+        lay_c(LAST + 2, "s")
+        lay_c(LAST + 1, "s")
+        turn(LAST - 1)
         row_max(LAST + 3)
         row_exp(LAST + 3)
+        y_copy(LAST - 1)
+        y_round(group_of[LAST - 1], nc.gpsimd)
         product(LAST)
         turn(LAST)
+        p_mm(LAST + 3, "z")
+        lay_c(LAST + 3, "s")
         invert(LAST + 2, 1)
         product(LAST + 1)
-        lay_c(LAST + 1, "s")
         turn(LAST + 1)
-        product(LAST + 2)
-        lay_c(LAST + 2, "z")
-        turn(LAST + 2)
         invert(LAST + 3, 1)
+        product(LAST + 2)
+        turn(LAST + 2)
         product(LAST + 3)
-        lay_c(LAST + 3, "s")
         turn(LAST + 3)
         y_copy(LAST + 0)
         y_round(group_of[LAST + 0], nc.gpsimd)
         y_copy(LAST + 1)
-        y_copy(LAST + 2)
+        y_copy(LAST + 2, nc.vector)
         y_copy(LAST + 3)
+        y_round_bank(LAST + 1, nc.scalar)
         y_round_bank(LAST + 2, nc.scalar)
-        y_round_bank(LAST + 1, nc.vector)
         y_quant(group_of[LAST - 4])
         y_quant(group_of[LAST - 2])
         y_quant(group_of[LAST - 1])
-        codes_store(LAST - 4, 4)
         y_store(LAST + 3, 1)
+        codes_store(LAST - 4, 4)
         y_quant(group_of[LAST + 0])
         y_round(group_of[LAST + 3], nc.vector)
         y_quant(group_of[LAST + 1])

@@ -182,12 +182,17 @@ def tile_laatlabelwisetokenevidence_x2_kernel(
             round_at[pair] = len(groups)
             groups.append((done, n))
             done = done + n
-        groups.extend([(u, 1) for u in range(done, NU)])
+        groups.append((done, 2))
+        groups.extend([(u, 1) for u in range(done + 2, NU)])
         assert done + 6 == NU
         group_of, y32 = {}, {}
+        y_last = const.tile([P, 4, 2 * P], F32, name="y_last")
         for gi in range(len(groups)):
             u0, n = groups[gi]
-            y32[gi] = const.tile([P, 4, n * P], F32, name="y32_%d" % gi)
+            if u0 < NU - 2:
+                y32[gi] = const.tile([P, 4, n * P], F32, name="y32_%d" % gi)[:]
+            else:
+                y32[gi] = y_last[:, :, P * (u0 - NU + 2) : P * (u0 - NU + 3)]
             for u in range(u0, u0 + n):
                 group_of[u] = gi
 
@@ -287,7 +292,7 @@ def tile_laatlabelwisetokenevidence_x2_kernel(
                 y_store(u, 1)
             elif u < SINGLES and k % 2 == 1:
                 y_store(u - 1, 2)
-            elif SINGLES <= u < NU - 1:
+            elif SINGLES <= u < NU - 2:
                 y_store(u, 1)
 
         def y_store(u, n):
@@ -299,7 +304,7 @@ def tile_laatlabelwisetokenevidence_x2_kernel(
 
         def y_round(gi, eng):
             n = groups[gi][1]
-            src = y32[gi][:].rearrange("p t (c i) -> p c t i", i=4)
+            src = y32[gi].rearrange("p t (c i) -> p c t i", i=4)
             if eng is nc.gpsimd:
                 tag, bufs = ("y16", 1) if n >= 2 else ("y16_last", 6)
                 y16[gi] = stage.tile([P, n * P, 4], BF16, name=tag, tag=tag, bufs=bufs, align_bytes=64)
@@ -570,47 +575,46 @@ def tile_laatlabelwisetokenevidence_x2_kernel(
 
         y_round(group_of[LAST - 4], nc.gpsimd)
         y_copy(LAST - 2)
-        y_round(group_of[LAST - 2], nc.gpsimd)
         row_exp(LAST + 2)
-        p_mm(LAST + 2)
         lay_c(LAST - 1, "t")
+        turn(LAST - 1)
+        p_mm(LAST + 2)
         lay_c(LAST, "t")
         lay_c(LAST + 2, "s")
         lay_c(LAST + 1, "s")
-        turn(LAST - 1)
+        y_copy(LAST - 1)
         row_max(LAST + 3)
         row_exp(LAST + 3)
-        y_copy(LAST - 1)
-        y_round(group_of[LAST - 1], nc.gpsimd)
         product(LAST)
         turn(LAST)
-        p_mm(LAST + 3, "z")
-        lay_c(LAST + 3, "s")
         invert(LAST + 2, 1)
         product(LAST + 1)
         turn(LAST + 1)
+        p_mm(LAST + 3, "z")
+        lay_c(LAST + 3, "s")
+        y_quant(group_of[LAST - 4])
+        codes_store(LAST - 4, 2)
+        y_round(group_of[LAST - 2], nc.gpsimd)
         invert(LAST + 3, 1)
         product(LAST + 2)
         turn(LAST + 2)
         product(LAST + 3)
         turn(LAST + 3)
         y_copy(LAST + 0)
-        y_round(group_of[LAST + 0], nc.gpsimd)
         y_copy(LAST + 1)
-        y_copy(LAST + 2, nc.vector)
+        y_round_bank(LAST + 0, nc.scalar)
+        y_copy(LAST + 2)
         y_copy(LAST + 3)
-        y_round_bank(LAST + 1, nc.scalar)
         y_round_bank(LAST + 2, nc.scalar)
-        y_quant(group_of[LAST - 4])
         y_quant(group_of[LAST - 2])
-        y_quant(group_of[LAST - 1])
-        y_store(LAST + 3, 1)
-        codes_store(LAST - 4, 4)
         y_quant(group_of[LAST + 0])
+        codes_store(LAST - 2, 3)
+        dst = out_0[B - 1].rearrange("(p t) l -> p t l", t=4)
+        nc.sync.dma_start(out=dst[:, :, L - 2 * P :], in_=y_last[:])
+        y_round(group_of[LAST + 1], nc.vector)
         y_round(group_of[LAST + 3], nc.vector)
         y_quant(group_of[LAST + 1])
-        codes_store(LAST + 0, 2)
         y_quant(group_of[LAST + 3])
         y_quant(group_of[LAST + 2])
-        codes_store(LAST + 2, 2)
+        codes_store(LAST + 1, 3)
         scales_store(B - 1, [nc.scalar, nc.sync, nc.scalar, nc.sync])

from contextlib import ExitStack

import concourse.mybir as mybir
from concourse.masks import make_identity

B, T, D, A, L = 4, 512, 512, 512, 1024
P = 128
NT = T // P
NL = L // P
NU = B * NL

F32 = mybir.dt.float32
BF16 = mybir.dt.bfloat16
I32 = mybir.dt.int32
U8 = mybir.dt.uint8
FP8X4 = mybir.dt.float8_e4m3fn_x4
ACT = mybir.ActivationFunctionType
ALU = mybir.AluOpType
AX = mybir.AxisListType

BANKS = {"s": 3, "p": 2, "t": 2, "z": 1}
YB = 1
HELD = (4, 7)
VS = 40
BY_VECTOR = (3,)
SINGLES = 24
FLOPS = 2 * B * T * (D * A + A * L + D * L)


def tile_laatlabelwisetokenevidence_x2_kernel(
    tc, h, w_words, w_scales, g, u_words, u_scales, beta_words, beta_scales, c, out_0, out_1, out_2
):
    nc = tc.nc
    out_words = out_1[0].rearrange("p m t -> p (m t)")

    with ExitStack() as ctx:
        const = ctx.enter_context(tc.tile_pool(name="const", bufs=1))
        stage = ctx.enter_context(tc.tile_pool(name="stage", bufs=4))
        stats = ctx.enter_context(tc.tile_pool(name="stats", bufs=4))
        psum = ctx.enter_context(tc.psum_pool(name="psum", bufs=2))
        ctx.enter_context(tc.manual_schedule())

        h_sb = {}

        def load_h(i, n):
            b, t_i = divmod(i, NT)
            rows = const.tile([P, n, D], BF16, name="h_sb_%d" % i, align_bytes=64)
            src = h[b].rearrange("(p t) d -> p t d", t=NT)
            nc.sync.dma_start(out=rows[:], in_=src[:, t_i : t_i + n, :])
            for d in range(n):
                h_sb[i + d] = rows[:].bitcast(F32)[:, d, :]

        w_raw = const.tile([P, A], I32, name="w_raw", align_bytes=64)
        ws_raw = const.tile([P, A], U8, name="ws_raw", align_bytes=64)
        u_sb = const.tile([P, L], I32, name="u_sb", align_bytes=64)
        us_sb = const.tile([P, L], U8, name="us_sb", align_bytes=64)
        b_sb = const.tile([P, L], I32, name="b_sb", align_bytes=64)
        bs_sb = const.tile([P, L], U8, name="bs_sb", align_bytes=64)
        g_bf = const.tile([P, 4], BF16, name="g_bf")
        c_row = const.tile([P, L], BF16, name="c_row", align_bytes=64)
        spread = const.tile([P, P], BF16, name="spread", align_bytes=64)
        ident = const.tile([P, P], F32, name="ident", align_bytes=64)
        nc.vector.memset(ws_raw[:].bitcast(I32), 0)
        nc.vector.memset(ident[:], 0.0)
        nc.vector.memset(c_row[:], 0.0)
        nc.vector.memset(us_sb[:].bitcast(I32), 0)
        nc.vector.memset(bs_sb[:].bitcast(I32), 0)
        nc.vector.memset(spread[:], 1.0 / T)

        def load_scales(eng, dst, src):
            for r in range(4):
                eng.dma_start(out=dst[r:P:32, :].bitcast(I32), in_=src[0, r:16:4, :].bitcast(I32))

        load_h(0, 1)
        nc.sync.dma_start(out=w_raw[:], in_=w_words[0].rearrange("p n t -> p (n t)").bitcast(I32))
        load_scales(nc.sync, ws_raw, w_scales)
        load_h(1, 1)
        load_h(2, 2)
        nc.sync.dma_start(out=g_bf[:], in_=g.rearrange("(p t) -> p t", t=4))
        for i in range(NT, 3 * NT, 2):
            load_h(i, 2)
        nc.sync.dma_start(out=u_sb[:], in_=u_words[0].rearrange("p n t -> p (n t)").bitcast(I32))
        load_scales(nc.sync, us_sb, u_scales)
        nc.sync.dma_start(out=b_sb[:], in_=beta_words[0].rearrange("p n t -> p (n t)").bitcast(I32))
        load_scales(nc.sync, bs_sb, beta_scales)

        make_identity(nc, ident[:], nomemset=True)
        w_sb = const.tile([P, 4, P], I32, name="w_sb", align_bytes=64)
        ws_sb = const.tile([P, 4, P], U8, name="ws_sb", align_bytes=64)
        g_sb = const.tile([P, 4], F32, name="g_sb")

        def prep_w():
            nc.vector.tensor_copy(out=ws_sb[:], in_=ws_raw[:].rearrange("p (m t) -> p t m", t=4))
            nc.vector.tensor_copy(out=w_sb[:], in_=w_raw[:].rearrange("p (m t) -> p t m", t=4))

        h_codes, h_scales, z_codes, z_scales = {}, {}, {}, {}
        for b in range(B):
            h_codes[b] = const.tile([P, T], I32, name="h_codes_%d" % b, align_bytes=64)
            h_scales[b] = const.tile([P, T], U8, name="h_scales_%d" % b, align_bytes=64)
            z_codes[b] = const.tile([P, T], I32, name="z_codes_%d" % b, align_bytes=64)
            z_scales[b] = const.tile([P, T], U8, name="z_scales_%d" % b, align_bytes=64)
        h_bank, h_il, z_bank, z_t, z_b = {}, {}, {}, {}, {}

        def h_turn(i, n, tag):
            h_bank[i] = psum.tile([P, n, 2, P], F32, name="h_bank", tag=tag, bufs=BANKS[tag])
            for d in range(n):
                for e in range(2):
                    nc.tensor.transpose(h_bank[i][:, d, e, :], h_sb[i + d][:, e : D // 2 : 2], ident[:])

        def h_copy(i, n):
            h_il[i] = stage.tile([P, n, P, 4], BF16, name="h_il", tag="h_il", bufs=6, align_bytes=64)
            nc.scalar.copy(out=h_il[i][:].bitcast(F32), in_=h_bank[i][:].rearrange("m i e p -> m i p e"))

        def h_quant(i, n):
            b, t_i = divmod(i, NT)
            cols = slice(P * t_i, P * (t_i + n))
            nc.vector.quantize_mx(
                out=h_codes[b][:, cols].bitcast(FP8X4),
                scales=h_scales[b][:, cols],
                in_=h_il[i][:].rearrange("m i p t -> m (i p t)"),
            )

        def z_mm(i, tag):
            b, t_i = divmod(i, NT)
            cols = slice(P * t_i, P * (t_i + 1))
            z_bank[i] = psum.tile([P, 4, P], F32, name="z_bank", tag=tag, bufs=BANKS[tag])
            for t in range(4):
                nc.tensor.matmul_mx(
                    out=z_bank[i][:, t, :],
                    lhsT=w_sb[:, t, :].bitcast(FP8X4),
                    lhsT_scale=ws_sb[:, t, :],
                    rhs=h_codes[b][:, cols].bitcast(FP8X4),
                    rhs_scale=h_scales[b][:, cols],
                    start=True,
                    stop=True,
                )

        def z_span(i):
            return (i, 1) if i < 2 * NT else (i - i % 2, 2)

        def z_tanh(i):
            i0, n = z_span(i)
            if i == i0:
                z_t[i0] = stage.tile([P, n * P, 4], F32, name="z_t", tag="z_t")
            d = i - i0
            nc.scalar.activation(
                out=z_t[i0][:, P * d : P * (d + 1), :], in_=z_bank[i][:].rearrange("m t n -> m n t"), func=ACT.Tanh
            )

        def z_gain(i, eng, lo, hi):
            if i not in z_b:
                tag, bufs = ("y16", YB) if i in HELD else ("z_b", NT)
                z_b[i] = stage.tile([P, z_span(i)[1] * P, 4], BF16, name=tag, tag=tag, bufs=bufs, align_bytes=64)
            eng.tensor_tensor(
                out=z_b[i][:, lo:hi, :],
                in0=z_t[i][:, lo:hi, :],
                in1=g_sb[:].unsqueeze(1).to_broadcast([P, hi - lo, 4]),
                op=ALU.mult,
            )

        def z_quant(i):
            b, t_i = divmod(i, NT)
            cols = slice(P * t_i, P * (t_i + z_span(i)[1]))
            nc.vector.quantize_mx(
                out=z_codes[b][:, cols].bitcast(FP8X4),
                scales=z_scales[b][:, cols],
                in_=z_b[i][:].rearrange("m p t -> m (p t)"),
            )

        s_ps, p_ps, t_ps, neg, ex, vt, y16 = {}, {}, {}, {}, {}, {}, {}
        dsum = const.tile([P, NU], F32, name="dsum")
        rinv = const.tile([P, NU], F32, name="rinv")
        o_codes = const.tile([P, NU * P], I32, name="o_codes", align_bytes=64)
        o_scales = const.tile([P, NU * P], U8, name="o_scales", align_bytes=64)

        groups, round_at = [], {}
        done = 0
        for pair in range(2, NU // 2 - 1):
            if pair % 2 == 1 and pair + 6 < B * NT:
                continue
            n = min(4 if pair + 6 < B * NT else 3, 2 * pair - 2 - done)
            round_at[pair] = len(groups)
            groups.append((done, n))
            done = done + n
        groups.append((done, 2))
        groups.extend([(u, 1) for u in range(done + 2, NU)])
        assert done + 6 == NU
        group_of, y32 = {}, {}
        y_last = const.tile([P, 4, 2 * P], F32, name="y_last")
        for gi in range(len(groups)):
            u0, n = groups[gi]
            if u0 < NU - 2:
                y32[gi] = const.tile([P, 4, n * P], F32, name="y32_%d" % gi)[:]
            else:
                y32[gi] = y_last[:, :, P * (u0 - NU + 2) : P * (u0 - NU + 3)]
            for u in range(u0, u0 + n):
                group_of[u] = gi

        def s_mm(u, tag="s"):
            b, j = divmod(u, NL)
            cols = slice(P * j, P * (j + 1))
            s_ps[u] = psum.tile([P, T], F32, name="s_ps", tag=tag, bufs=BANKS[tag])
            nc.tensor.matmul_mx(
                out=s_ps[u][:],
                lhsT=u_sb[:, cols].bitcast(FP8X4),
                lhsT_scale=us_sb[:, cols],
                rhs=z_codes[b][:].bitcast(FP8X4),
                rhs_scale=z_scales[b][:],
                start=True,
                stop=True,
            )

        def p_mm(u, tag="p"):
            b, j = divmod(u, NL)
            cols = slice(P * j, P * (j + 1))
            p_ps[u] = psum.tile([P, T], F32, name="p_ps", tag=tag, bufs=BANKS[tag])
            nc.tensor.matmul_mx(
                out=p_ps[u][:],
                lhsT=b_sb[:, cols].bitcast(FP8X4),
                lhsT_scale=bs_sb[:, cols],
                rhs=h_codes[b][:].bitcast(FP8X4),
                rhs_scale=h_scales[b][:],
                start=True,
                stop=True,
            )

        def row_max(u):
            neg[u] = stats.tile([P, 1], F32, name="neg", tag="neg")
            nc.vector.tensor_reduce(out=neg[u][:], in_=s_ps[u][:], axis=AX.X, op=ALU.max, negate=True)

        def row_exp(u):
            ex[u] = stage.tile([P, T], F32, name="ex", tag="ex", bufs=5)
            nc.scalar.activation(
                out=ex[u][:], in_=s_ps[u][:], func=ACT.Exp, bias=neg[u][:], accum_out=dsum[:, u : u + 1]
            )

        def invert(u, n):
            nc.vector.reciprocal(out=rinv[:, u : u + n], in_=dsum[:, u : u + n])

        def product(u):
            vt[u] = stage.tile([P, T], F32, name="vt", tag="vt")
            nc.vector.scalar_tensor_tensor(
                out=vt[u][:], in0=p_ps[u][:], scalar=rinv[:, u : u + 1], in1=ex[u][:], op0=ALU.mult, op1=ALU.mult
            )

        def lay_c(u, tag):
            j = u % NL
            t_ps[u] = psum.tile([P, 4, P], F32, name="t_ps", tag=tag, bufs=BANKS[tag])
            if u in BY_VECTOR:
                return
            nc.tensor.matmul(
                out=t_ps[u][:],
                lhsT=spread[:],
                rhs=c_row[:, P * j : P * (j + 1)].unsqueeze(1).to_broadcast([P, 4, P]),
                start=True,
                stop=False,
            )

        def turn(u):
            for t in range(4):
                nc.tensor.matmul(
                    out=t_ps[u][:, t, :],
                    lhsT=vt[u][:, P * t : P * (t + 1)],
                    rhs=ident[:],
                    is_transpose=True,
                    start=(u in BY_VECTOR),
                    stop=(t == 3 or u in BY_VECTOR),
                )

        def y_copy(u, eng=nc.scalar):
            gi = group_of[u]
            u0, n = groups[gi]
            k = u - u0
            if u in BY_VECTOR:
                nc.vector.scalar_tensor_tensor(
                    out=y32[gi][:, :, P * k : P * (k + 1)],
                    in0=t_ps[u][:],
                    scalar=float(T),
                    in1=c_all[u % NL][:].unsqueeze(1).to_broadcast([P, 4, P]),
                    op0=ALU.mult,
                    op1=ALU.add,
                )
            elif eng is nc.vector:
                nc.vector.tensor_scalar(
                    out=y32[gi][:, :, P * k : P * (k + 1)], in0=t_ps[u][:], scalar1=float(T), scalar2=None, op0=ALU.mult
                )
            else:
                nc.scalar.activation(
                    out=y32[gi][:, :, P * k : P * (k + 1)], in_=t_ps[u][:], func=ACT.Copy, scale=float(T)
                )
            if u < SINGLES and n == 3 and k == 2:
                y_store(u, 1)
            elif u < SINGLES and k % 2 == 1:
                y_store(u - 1, 2)
            elif SINGLES <= u < NU - 2:
                y_store(u, 1)

        def y_store(u, n):
            gi = group_of[u]
            k = u - groups[gi][0]
            b, j = divmod(u, NL)
            dst = out_0[b].rearrange("(p t) l -> p t l", t=4)
            nc.sync.dma_start(out=dst[:, :, P * j : P * (j + n)], in_=y32[gi][:, :, P * k : P * (k + n)])

        def y_round(gi, eng):
            n = groups[gi][1]
            src = y32[gi].rearrange("p t (c i) -> p c t i", i=4)
            if eng is nc.gpsimd:
                tag, bufs = ("y16", 1) if n >= 2 else ("y16_last", 6)
                y16[gi] = stage.tile([P, n * P, 4], BF16, name=tag, tag=tag, bufs=bufs, align_bytes=64)
                dst = y16[gi][:].rearrange("p (c i) t -> p c t i", i=4)
                eng.tensor_scalar(out=dst, in0=src, scalar1=1.0, scalar2=1.0, op0=ALU.mult, op1=ALU.mult)
            else:
                y16[gi] = stage.tile([P, n * P, 4], BF16, name="y16_last", tag="y16_last", bufs=6, align_bytes=64)
                eng.tensor_copy(out=y16[gi][:].rearrange("p (c i) t -> p c t i", i=4), in_=src)

        def y_round_bank(u, eng):
            gi = group_of[u]
            y16[gi] = stage.tile([P, P, 4], BF16, name="y16_last", tag="y16_last", bufs=6, align_bytes=64)
            src = t_ps[u][:].rearrange("p t l -> p l t")
            if eng is nc.vector:
                eng.tensor_scalar(out=y16[gi][:], in0=src, scalar1=float(T), scalar2=None, op0=ALU.mult)
            else:
                eng.activation(out=y16[gi][:], in_=src, func=ACT.Copy, scale=float(T))

        def y_quant(gi):
            u0, n = groups[gi]
            cols = slice(P * u0, P * (u0 + n))
            nc.vector.quantize_mx(
                out=o_codes[:, cols].bitcast(FP8X4),
                scales=o_scales[:, cols],
                in_=y16[gi][:].rearrange("p l t -> p (l t)"),
            )

        def codes_store(u0, n):
            cols = slice(P * u0, P * (u0 + n))
            nc.sync.dma_start(out=out_words[:].bitcast(I32)[:, cols], in_=o_codes[:, cols])

        def scales_store(b, engines):
            for r in range(4):
                engines[r].dma_start(
                    out=out_2[0, 4 * r : 4 * r + 4, L * b : L * (b + 1)].bitcast(I32),
                    in_=o_scales[32 * r : 32 * r + 4, L * b : L * (b + 1)].bitcast(I32),
                )

        h_turn(0, 1, "t")
        h_turn(1, 1, "t")
        prep_w()
        h_turn(2, 1, "p")
        h_turn(3, 1, "p")
        for i in range(NT):
            h_copy(i, 1)
            h_quant(i, 1)
            z_mm(i, "s" if i < 3 else "z")
        nc.vector.tensor_copy(out=g_sb[:], in_=g_bf[:])
        nc.sync.dma_start(out=c_row[0:1, :], in_=c.rearrange("(o l) -> o l", o=1))
        for i in range(3 * NT, B * NT, 2):
            load_h(i, 2)
        c_all = {}
        for j in sorted(set(u % NL for u in BY_VECTOR)):
            c_all[j] = const.tile([P, P], BF16, name="c_all_%d" % j, align_bytes=64)
            nc.sync.dma_start(out=c_all[j][:], in_=c[P * j : P * (j + 1)].partition_broadcast(P))
        for i in range(NT):
            z_tanh(i)
        h_turn(4, 2, "t")
        h_turn(6, 2, "t")
        h_copy(4, 2)
        h_copy(6, 2)
        h_turn(8, 2, "p")
        h_turn(10, 2, "p")
        h_copy(8, 2)
        h_copy(10, 2)
        for i in range(NT):
            if i == NT - 1:
                h_quant(4, 2)
            z_gain(i, nc.vector, 0, P)
            if i > 0:
                z_quant(i - 1)
        z_quant(NT - 1)
        for i in range(6, 3 * NT, 2):
            h_quant(i, 2)
        for i in (4, 5):
            z_mm(i, "t")
            z_tanh(i)
        s_mm(0)
        z_mm(6, "z")
        z_tanh(6)
        s_mm(1)
        s_mm(2)
        for u in range(3):
            row_max(u)
        p_mm(0)
        s_mm(3, "t")
        row_exp(0)
        row_exp(1)

        def unit(u):
            return 0 <= u < NU

        LAST = NU - 4
        AHEAD = 22

        def p_bank(u):
            return "z" if (u - AHEAD) % 3 == 0 else "p"

        def y_out(gi):
            y_quant(gi)
            u0, n = groups[gi]
            codes_store(u0, n)
            if (u0 + n) // NL > u0 // NL:
                scales_store(u0 // NL, [nc.sync] * 4)

        def share(j):
            return 0 if j == 1 or 4 * j - 1 in BY_VECTOR else VS

        for k in range(4):
            pair, second = divmod(k, 2)
            if k == 0:
                for i in (4, 5, 6):
                    z_gain(i, nc.gpsimd, 0, P)
            if k == 2:
                z_gain(7, nc.gpsimd, 0, P)
            if second:
                row_exp(k + 2)
            if k == 1:
                z_tanh(7)
            if unit(k - 2):
                y_copy(k - 2)
            if not second:
                row_exp(k + 2)
                if k == 2:
                    h_copy(12, 2)
                p_mm(k + 1)
                if pair == 0:
                    s_mm(k + 4)
                z_mm(pair + 7, "z")
                if pair > 0:
                    s_mm(k + 4)
                if pair > 0:
                    z_tanh(pair + 7)
                for u in (k - 1, k):
                    if unit(u):
                        lay_c(u, "t")
                if unit(k - 1):
                    turn(k - 1)
                else:
                    h_turn(12, 2, "s")
            elif k == 1:
                turn(k - 1)
                p_mm(k + 1)
                s_mm(k + 4)
            else:
                turn(k - 1)
                s_mm(k + 4)
                p_mm(k + 1)
                z_mm(9, "z")
            if k == 0:
                invert(0, 1)
                row_max(3)
                product(0)
                invert(1, 1)
            if k > 0:
                row_max(k + 3)
            if k > 0:
                product(k)
            if k == 1:
                for i in (4, 5, 6):
                    z_quant(i)
            if k == 3:
                z_quant(7)
                h_quant(12, 2)
            if second:
                invert(k + 1, 2)
        row_exp(6)
        z_tanh(9)
        p_mm(5)
        s_mm(8)
        lay_c(3, "t")
        turn(3)

        for j in range(1, B + 1):
            k = 4 * j
            z_i = 2 * j + 6
            h_i = 2 * j + 12
            y_round(round_at[2 * j], nc.gpsimd)
            row_max(k + 3)
            if j > 1:
                z_tanh(z_i + 1)
            z_gain(z_i, nc.gpsimd, share(j), 2 * P)
            row_exp(k + 3)
            product(k)
            if k - 2 not in BY_VECTOR:
                y_copy(k - 2)
            if h_i < B * NT:
                h_turn(h_i, 2, "z")
            s_mm(k + 5)
            p_mm(k + 2)
            row_max(k + 4)
            product(k + 1)
            if k - 1 not in BY_VECTOR:
                y_copy(k - 1)
            if h_i < B * NT:
                h_copy(h_i, 2)
            row_exp(k + 4)
            for u in (k - 2, k - 1):
                if u in BY_VECTOR:
                    y_copy(u)
            invert(k + 2, 2)
            s_mm(k + 6)
            p_mm(k + 3)
            if j < B:
                z_mm(z_i + 2, "z")
            lay_c(k, "t")
            lay_c(k + 1, "t")
            turn(k)
            turn(k + 1)
            row_max(k + 5)
            if j == 1:
                z_tanh(z_i + 2)
                z_gain(z_i + 2, nc.gpsimd, 0, VS)
            row_exp(k + 5)
            if 1 < j < B:
                z_tanh(z_i + 2)
            product(k + 2)
            row_max(k + 6)
            product(k + 3)
            y_copy(k)
            y_copy(k + 1)
            row_exp(k + 6)
            y_out(round_at[2 * j])
            z_quant(z_i)
            if h_i < B * NT:
                h_quant(h_i, 2)
            if 1 < j < B and share(j + 1) > 0:
                z_gain(z_i + 2, nc.vector, 0, VS)
            invert(k + 4, 2)
            s_mm(k + 7)
            p_mm(k + 4)
            if j < B:
                z_mm(z_i + 3, "z")
            p_mm(k + 5)
            if j < B:
                s_mm(k + 8)
            last = k + 3 if j < B else k + 2
            for u in range(k + 2, last + 1):
                lay_c(u, "t")
            for u in range(k + 2, last + 1):
                turn(u)

        FIRST = 4 * B + 4
        for k in range(FIRST, LAST):
            pair, second = divmod(k, 2)
            if not second:
                y_round(round_at[pair], nc.gpsimd)
            else:
                row_exp(k + 2)
            y_copy(k - 2)
            if not second:
                if k > FIRST:
                    row_exp(k + 2)
                p_mm(k + 2, p_bank(k + 2))
                s_mm(k + 4)
                lay_c(k - 1, "t")
                lay_c(k, "t")
                turn(k - 1)
            else:
                turn(k - 1)
                s_mm(k + 4)
                p_mm(k + 2, p_bank(k + 2))
            row_max(k + 3)
            product(k)
            if second:
                y_out(round_at[pair])
                invert(k + 1, 2)

        y_round(group_of[LAST - 4], nc.gpsimd)
        y_copy(LAST - 2)
        row_exp(LAST + 2)
        lay_c(LAST - 1, "t")
        turn(LAST - 1)
        p_mm(LAST + 2)
        lay_c(LAST, "t")
        lay_c(LAST + 2, "s")
        lay_c(LAST + 1, "s")
        y_copy(LAST - 1)
        row_max(LAST + 3)
        row_exp(LAST + 3)
        product(LAST)
        turn(LAST)
        invert(LAST + 2, 1)
        product(LAST + 1)
        turn(LAST + 1)
        p_mm(LAST + 3, "z")
        lay_c(LAST + 3, "s")
        y_quant(group_of[LAST - 4])
        codes_store(LAST - 4, 2)
        y_round(group_of[LAST - 2], nc.gpsimd)
        invert(LAST + 3, 1)
        product(LAST + 2)
        turn(LAST + 2)
        product(LAST + 3)
        turn(LAST + 3)
        y_copy(LAST + 0)
        y_copy(LAST + 1)
        y_round_bank(LAST + 0, nc.scalar)
        y_copy(LAST + 2)
        y_copy(LAST + 3)
        y_round_bank(LAST + 2, nc.scalar)
        y_quant(group_of[LAST - 2])
        y_quant(group_of[LAST + 0])
        codes_store(LAST - 2, 3)
        dst = out_0[B - 1].rearrange("(p t) l -> p t l", t=4)
        nc.sync.dma_start(out=dst[:, :, L - 2 * P :], in_=y_last[:])
        y_round(group_of[LAST + 1], nc.vector)
        y_round(group_of[LAST + 3], nc.vector)
        y_quant(group_of[LAST + 1])
        y_quant(group_of[LAST + 3])
        y_quant(group_of[LAST + 2])
        codes_store(LAST + 1, 3)
        scales_store(B - 1, [nc.scalar, nc.sync, nc.scalar, nc.sync])
